import numpy as np
import ml_dtypes


def mxq(x, axis, fmt="e4m3"):
    dtype, down = {"e4m3": (ml_dtypes.float8_e4m3fn, 7), "e5m2": (ml_dtypes.float8_e5m2, 14)}[fmt]
    v = np.moveaxis(np.asarray(x, np.float32).astype(ml_dtypes.bfloat16).astype(np.float64), axis, -1)
    blocks = v.reshape(v.shape[:-1] + (-1, 32))
    amax = np.abs(blocks).max(-1, keepdims=True)
    byte = np.maximum(np.where(amax > 0, np.frexp(amax)[1] - 1 + 127, 0) - down, 1)
    scale = np.exp2(byte - 127.0)
    codes = (blocks / scale).astype(np.float32).astype(dtype).astype(np.float64)
    return np.moveaxis((codes * scale).reshape(v.shape), -1, axis)


WIDE = False


def mx_kscale(k):
    if not WIDE:
        return np.ones(k)
    levels = np.array([10, -10, 5, -5, 0])
    if k % 512:
        return np.exp2(np.random.permutation(np.resize(levels, k // 32))).repeat(32)
    a = np.empty((k // 512, 16))
    for p in range(k // 512):
        a[p, :8] = np.random.permutation(np.resize(levels, 8))
        for g in range(8):
            far = levels[np.abs(levels - a[p, g]) >= 10]
            a[p, g + 8] = far[np.random.randint(len(far))]
    return np.exp2(a.ravel()).repeat(32)


def f64(x):
    return np.asarray(x).astype(np.float64)


def striped(idx):
    return np.tile(idx.reshape(-1, 16).T, (8, 1)).astype(np.uint16)


def unstriped(offs):
    return offs[:16].T.reshape(-1).astype(np.int64)


E2M1 = np.array([0.0, 0.5, 1.0, 1.5, 2.0, 3.0, 4.0, 6.0, -0.0, -0.5, -1.0, -1.5, -2.0, -3.0, -4.0, -6.0])


def pack_weight(w, fmt):
    k, n = w.shape
    w = f64(np.asarray(w, np.float32).astype(ml_dtypes.bfloat16)).reshape(k // 32, 32, n)
    amax = np.abs(w).max(1)
    if fmt == "e4m3":
        byte = np.frexp(amax)[1] - 1 + 127 - 7
    else:
        mant, ex = np.frexp(amax / 6.0)
        byte = np.where(mant > 0.5, ex, ex - 1) + 127
    byte = np.clip(np.where(amax > 0, byte, 1), 1, 254)
    scaled = (w * np.exp2(127.0 - byte)[:, None, :]).reshape(k, n).astype(np.float32)
    by_word = np.ascontiguousarray(scaled.reshape(k // 512, 128, 4, n).transpose(0, 1, 3, 2))
    if fmt == "e4m3":
        words = by_word.astype(ml_dtypes.float8_e4m3fn).view(np.uint8)
    else:
        c = by_word.astype(ml_dtypes.float4_e2m1fn).view(np.uint8) & 0xF
        words = (c[..., 0::2] | (c[..., 1::2] << 4)).reshape(k // 512, 128, 2 * n)
    return np.ascontiguousarray(words), np.ascontiguousarray(byte.astype(np.uint8).reshape(k // 512, 16, n))


def unpack_weight(words, scales, fmt):
    g, _, n = scales.shape
    words = np.ascontiguousarray(words).reshape(g, 128, n, -1)
    if fmt == "e4m3":
        vals = words.view(ml_dtypes.float8_e4m3fn).astype(np.float64)
    else:
        nib = np.empty((g, 128, n, 4), np.uint8)
        nib[..., 0::2] = words & 0xF
        nib[..., 1::2] = words >> 4
        vals = E2M1[nib]
    vals = vals * np.repeat(np.exp2(scales.astype(np.float64) - 127.0), 8, axis=1)[..., None]
    return vals.transpose(0, 1, 3, 2).reshape(g * 512, n)


def gelu(v):
    return 0.5 * v * (1.0 + np.tanh(np.sqrt(2.0 / np.pi) * (v + 0.044715 * v**3)))


K, T, S, H, P, N, P2 = 1024, 2048, 1024, 1024, 512, 512, 256

def setup_inputs():
    n = np.random.standard_normal
    s = mx_kscale(K)[:, None]
    u = mx_kscale(H)[:, None]
    tab_words, tab_scales = pack_weight(n((K, T)) * s, "e4m3")
    w1 = (1.5 * n((K, H)) / np.sqrt(K) / s).astype(np.float32)
    gain = (np.exp(0.3 * n(H)) * u[:, 0]).astype(np.float32)
    w2_words, w2_scales = pack_weight(4.0 * n((H, N)) / np.sqrt(H) / u, "e2m1")
    return {
        "tab_words": tab_words, "tab_scales": tab_scales,
        "w1": w1, "gain": gain,
        "w2_words": w2_words, "w2_scales": w2_scales,
        "offs": striped(np.random.permutation(T)[:S]),
        "pos1": striped(np.random.permutation(S)[:P]),
        "pos2": striped(np.random.permutation(S)[:P]),
        "pos3": striped(np.random.permutation(P)[:P2]),
        "pos4": striped(np.random.permutation(P)[:P2]),
    }

def reference(tab_words, tab_scales, w1, gain, w2_words, w2_scales, offs, pos1, pos2, pos3, pos4):
    v = unpack_weight(tab_words, tab_scales, "e4m3")[:, unstriped(offs)]
    w1q = mxq(f64(w1), 0, "e4m3")
    w2 = unpack_weight(w2_words, w2_scales, "e2m1")
    d = w1q.T @ v
    h = 1.0 / (1.0 + np.exp(-d))
    both = h[:, unstriped(pos1)] * h[:, unstriped(pos2)]
    z = both * f64(gain)[:, None]
    zq = mxq(z, 0, "e4m3")
    e = w2.T @ zq
    y = 1.0 / (1.0 + np.exp(-e))
    left = y[:, unstriped(pos3)]
    right = y[:, unstriped(pos4)]
    out = left * (1.0 - right)
    return out

@@ -1,0 +1,266 @@
+from contextlib import ExitStack
+
+import concourse.mybir as mybir
+
+F32 = mybir.dt.float32
+BF16 = mybir.dt.bfloat16
+I32 = mybir.dt.int32
+U32 = mybir.dt.uint32
+U16 = mybir.dt.uint16
+U8 = mybir.dt.uint8
+FP8X4 = mybir.dt.float8_e4m3fn_x4
+FP4X4 = mybir.dt.float4_e2m1fn_x4
+MULT = mybir.AluOpType.mult
+SIGMOID = mybir.ActivationFunctionType.Sigmoid
+
+P = 128
+K, T, S, H, M, N, J = 1024, 2048, 1024, 1024, 512, 512, 256
+BANK = 512
+FLOPS = 2 * K * H * S + 2 * H * N * M
+
+
+def tile_list_boolean_tree_retrieval_kernel(
+    tc, tab_words, tab_scales, w1, gain, w2_words, w2_scales, offs, pos1, pos2, pos3, pos4, out
+):
+    nc = tc.nc
+    with ExitStack() as ctx:
+        sb = ctx.enter_context(tc.tile_pool(name="sb", bufs=1))
+        ps = ctx.enter_context(tc.psum_pool(name="ps", bufs=1))
+
+        def tile(shape, dtype, name, tag=None):
+            return sb.tile(shape, dtype, name=name, tag=tag or name, align_bytes=64)
+
+        def load_list(src, name):
+            t = sb.tile(list(src.shape), U16, name=name)
+            nc.sync.dma_start(t[:], src)
+            return t
+
+        tab_sc = tile([P, T], U8, "tab_sc")
+        nc.vector.memset(tab_sc[:].bitcast(I32), 0)
+        w2_sc = tile([P, 2, N], U8, "w2_sc")
+        nc.vector.memset(w2_sc[:].rearrange("p a n -> p (a n)").bitcast(I32), 0)
+
+        offs_t = load_list(offs, "offs_t")
+
+        tab_w = [tile([P, T], I32, "tab_w%d" % a) for a in range(2)]
+        raw = {}
+
+        def load_tab(a):
+            nc.sync.dma_start(tab_w[a][:], tab_words[a].rearrange("p t i -> p (t i)").bitcast(I32))
+
+        def load_w1(b, a, half):
+            raw[b, a, half] = tile([P, 4, 256], F32, "raw%d%d%d" % (b, a, half))
+            c0 = 512 * b + 256 * half
+            nc.sync.dma_start(
+                raw[b, a, half][:], w1[512 * a : 512 * a + 512, c0 : c0 + 256].rearrange("(p j) c -> p j c", j=4)
+            )
+
+        load_w1(0, 0, 0)
+        for q in range(4):
+            nc.sync.dma_start(
+                tab_sc[32 * q : 32 * q + 8, :].bitcast(I32), tab_scales[:, 4 * q : 4 * q + 4, :].bitcast(I32)
+            )
+        load_tab(0)
+        gain_t = tile([P, 2, 4], F32, "gain_t")
+        nc.sync.dma_start(gain_t[:], gain.rearrange("(b p t) -> p b t", b=2, t=4))
+        load_w1(0, 0, 1)
+        load_tab(1)
+        load_w1(0, 1, 0)
+        load_w1(0, 1, 1)
+        pos1_t = load_list(pos1, "pos1_t")
+        pos2_t = load_list(pos2, "pos2_t")
+        for a in range(2):
+            for half in range(2):
+                load_w1(1, a, half)
+        w2_w = tile([P, 2, 2 * N], U8, "w2_w")
+        nc.sync.dma_start(w2_w[:].bitcast(I32), w2_words.rearrange("a p c -> p a c").bitcast(I32))
+        for q in range(4):
+            nc.sync.dma_start(
+                w2_sc[32 * q : 32 * q + 4, :, :].bitcast(I32),
+                w2_scales[:, 4 * q : 4 * q + 4, :].rearrange("a r c -> r a c").bitcast(I32),
+            )
+        pos3_t = load_list(pos3, "pos3_t")
+        pos4_t = load_list(pos4, "pos4_t")
+
+        warm = tile([P, 1], F32, "warm")
+        nc.scalar.activation(warm[:], gain_t[:, 0, 0:1], SIGMOID)
+
+        v_sc = tile([P, S], U8, "v_sc")
+        v_w = [tile([P, S], U32, "v_w%d" % a) for a in range(2)]
+        w_bf = {(b, a): tile([P, 2048], BF16, "w_bf%d%d" % (b, a)) for b in range(2) for a in range(2)}
+        w_code = {(b, a): tile([P, 512], U32, "w_code%d%d" % (b, a)) for b in range(2) for a in range(2)}
+        w_sc = {(b, a): tile([P, 512], U8, "w_sc%d%d" % (b, a)) for b in range(2) for a in range(2)}
+
+        def cast_w1(b, a, half, on_vector, m0=0, m1=64):
+            dst = w_bf[b, a][:].rearrange("p (t m j) -> p m j t", t=4, j=4)[:, 64 * half + m0 : 64 * half + m1]
+            src = raw[b, a, half][:].rearrange("p j (m t) -> p m j t", t=4)[:, m0:m1]
+            if on_vector:
+                nc.vector.tensor_copy(dst, src)
+            else:
+                nc.scalar.copy(dst, src)
+
+        def quant_w1(b, a, t0, t1):
+            nc.vector.quantize_mx(
+                w_code[b, a][:, 128 * t0 : 128 * t1].bitcast(FP8X4),
+                w_sc[b, a][:, 128 * t0 : 128 * t1],
+                w_bf[b, a][:, 512 * t0 : 512 * t1],
+            )
+
+        banks = {}
+
+        def first_pass(b, t, a):
+            for s in range(2):
+                if a == 0:
+                    banks[b, t, s] = ps.tile([P, BANK], F32, name="d%d%d%d" % (b, t, s), tag="bank%d" % (2 * t + s))
+                cols = slice(BANK * s, BANK * (s + 1))
+                nc.tensor.matmul_mx(
+                    banks[b, t, s][:],
+                    lhsT=w_code[b, a][:, 128 * t : 128 * (t + 1)].bitcast(FP8X4),
+                    lhsT_scale=w_sc[b, a][:, 128 * t : 128 * (t + 1)],
+                    rhs=v_w[a][:, cols].bitcast(FP8X4),
+                    rhs_scale=v_sc[4 * a : P, cols],
+                    start=(a == 0),
+                    stop=(a == 1),
+                )
+
+        h = {}
+
+        def sigmoid_h(b, t):
+            h[b, t] = tile([P, S], F32, "h%d%d" % (b, t))
+            for s in range(2):
+                nc.scalar.activation(h[b, t][:, BANK * s : BANK * (s + 1)], banks[b, t, s][:], SIGMOID)
+
+        nc.vector.tensor_copy(v_sc[:], tab_sc[:].indirect(offs_t[:]))
+        nc.vector.tensor_copy(v_w[0][:], tab_w[0][:].bitcast(U32).indirect(offs_t[:]))
+        cast_w1(0, 0, 0, False)
+        cast_w1(0, 0, 1, False)
+        quant_w1(0, 0, 0, 4)
+        nc.vector.tensor_copy(v_w[1][:], tab_w[1][:].bitcast(U32).indirect(offs_t[:]))
+        for t in range(4):
+            first_pass(0, t, 0)
+        cast_w1(0, 1, 0, False)
+        cast_w1(0, 1, 1, False, 0, 24)
+        cast_w1(0, 1, 1, True, 24, 64)
+        quant_w1(0, 1, 0, 1)
+        quant_w1(0, 1, 1, 2)
+        quant_w1(0, 1, 2, 4)
+        for t in range(4):
+            first_pass(0, t, 1)
+        cast_w1(1, 0, 0, True)
+
+        z0 = tile([P, 4 * M], F32, "z0")
+        z1a = tile([P, 4 * M], F32, "z1a")
+        gain_first = tile([P, M], F32, "gain_first")
+        gain_last = tile([P, 256], F32, "gain_last", tag="z1bc")
+        spread = [gain_first[:]] + [z0[:, M * u : M * (u + 1)] for u in range(4)]
+        spread = spread + [z1a[:, 0:M], z1a[:, M : 2 * M], z1a[:, 2 * M : 2 * M + 256]]
+        for u in range(8):
+            width = spread[u].shape[1]
+            nc.scalar.copy(spread[u], gain_t[:, u // 4, u % 4 : u % 4 + 1].to_broadcast([P, width]))
+        nc.scalar.copy(gain_last[:], gain_t[:, 1, 3:4].to_broadcast([P, 256]))
+
+        left = {}
+
+        def gather_left(u, tag=None):
+            left[u] = tile([P, M], F32, "left%d" % u, tag=tag)
+            nc.vector.tensor_tensor(left[u][:], h[u // 4, u % 4][:].indirect(pos1_t[:]), spread[u], MULT)
+
+        def gather_right(u, dst, m0, m1):
+            nc.vector.tensor_tensor(
+                dst, h[u // 4, u % 4][:].indirect(pos2_t[:, m0 // 16 : m1 // 16]), left[u][:, m0:m1], MULT
+            )
+
+        z_bf = {}
+
+        def weave(name, planes, width):
+            z_bf[name] = tile([P, 4 * width], BF16, "zbf" + name)
+            nc.scalar.copy(
+                z_bf[name][:].rearrange("p (c i t) -> p c t i", i=4, t=4),
+                planes.rearrange("p t (c i) -> p c t i", i=4),
+            )
+
+        sigmoid_h(0, 0)
+        sigmoid_h(0, 1)
+        gather_left(0)
+        gather_left(1)
+        cast_w1(1, 0, 1, False)
+        gather_right(0, z0[:, 0:M], 0, M)
+        sigmoid_h(0, 2)
+        quant_w1(1, 0, 0, 4)
+        gather_left(2, "w_bf10")
+        cast_w1(1, 1, 0, False)
+        cast_w1(1, 1, 1, False)
+        gather_right(1, z0[:, M : 2 * M], 0, M)
+        sigmoid_h(0, 3)
+        quant_w1(1, 1, 0, 4)
+        for t in range(4):
+            first_pass(1, t, 0)
+        for t in range(4):
+            first_pass(1, t, 1)
+        gather_left(3, "w_bf11")
+        gather_right(2, z0[:, 2 * M : 3 * M], 0, M)
+        for t in range(4):
+            sigmoid_h(1, t)
+        gather_left(4)
+        gather_right(3, z0[:, 3 * M : 4 * M], 0, M)
+        weave("0", z0[:].rearrange("p (t m) -> p t m", t=4), M)
+        gather_left(5)
+        gather_right(4, z1a[:, 0:256], 0, 256)
+        gather_left(6)
+        gather_right(5, z1a[:, M : M + 256], 0, 256)
+        left[7] = tile([P, M], F32, "left7")
+        nc.vector.tensor_tensor(left[7][:, 0:256], h[1, 3][:].indirect(pos1_t[:, 0:16]), spread[7], MULT)
+        gather_right(6, z1a[:, 2 * M : 2 * M + 256], 0, 256)
+        nc.vector.tensor_tensor(left[7][:, 256:512], h[1, 3][:].indirect(pos1_t[:, 16:32]), gain_last[:], MULT)
+        gather_right(7, z1a[:, 3 * M : 3 * M + 256], 0, 256)
+        weave("1a", z1a[:].rearrange("p (t m) -> p t m", t=4)[:, :, 0:256], 256)
+        z1bc = tile([P, 2 * M], F32, "z1bc")
+        for c in range(2):
+            for t in range(4):
+                o = M * c + 128 * t
+                gather_right(4 + t, z1bc[:, o : o + 128], 256 + 128 * c, 384 + 128 * c)
+            weave("1" + "bc"[c], z1bc[:, M * c : M * (c + 1)].rearrange("p (t m) -> p t m", t=4), 128)
+
+        z_code = [tile([P, M], U32, "z_code0", tag="left4"), tile([P, M], U32, "z_code1")]
+        z_sc = [tile([P, M], U8, "z_sc%d" % a) for a in range(2)]
+
+        def quant_z(a, name, m0, m1):
+            nc.vector.quantize_mx(z_code[a][:, m0:m1].bitcast(FP8X4), z_sc[a][:, m0:m1], z_bf[name][:])
+
+        quant_z(0, "0", 0, M)
+        quant_z(1, "1a", 0, 256)
+        quant_z(1, "1b", 256, 384)
+        quant_z(1, "1c", 384, 512)
+
+        def second_pass(bank, n, a, m0, m1, stop):
+            nc.tensor.matmul_mx(
+                bank[:, m0:m1],
+                lhsT=w2_w[:, a, 256 * n : 256 * (n + 1)].bitcast(FP4X4),
+                lhsT_scale=w2_sc[:, a, 128 * n : 128 * (n + 1)],
+                rhs=z_code[a][:, m0:m1].bitcast(FP8X4),
+                rhs_scale=z_sc[a][:, m0:m1],
+                start=(a == 0),
+                stop=stop,
+            )
+
+        y, not_y, right = {}, {}, {}
+        for n in range(4):
+            bank = ps.tile([P, BANK], F32, name="e%d" % n, tag="bank%d" % n)
+            second_pass(bank, n, 0, 0, M, False)
+            if n == 0:
+                for c in range(4):
+                    second_pass(bank, n, 1, 128 * c, 128 * (c + 1), c == 3)
+            else:
+                second_pass(bank, n, 1, 0, M, True)
+            not_y[n] = tile([P, M], F32, "not_y%d" % n)
+            y[n] = tile([P, M], F32, "y%d" % n)
+            nc.scalar.activation(not_y[n][:], bank[:], SIGMOID, scale=-1.0)
+            nc.scalar.activation(y[n][:], bank[:], SIGMOID)
+        for n in range(5):
+            if n < 4:
+                right[n] = tile([P, J], F32, "right%d" % n)
+                nc.vector.tensor_copy(right[n][:], not_y[n][:].indirect(pos4_t[:]))
+            if n > 0:
+                res = tile([P, J], F32, "res%d" % (n - 1))
+                nc.vector.tensor_tensor(res[:], y[n - 1][:].indirect(pos3_t[:]), right[n - 1][:], MULT)
+                nc.sync.dma_start(out[P * (n - 1) : P * n, :], res[:])

@@ -36,7 +36,7 @@ def tile_list_boolean_tree_retrieval_kernel(
             return t
 
         tab_sc = tile([P, T], U8, "tab_sc")
-        nc.vector.memset(tab_sc[:].bitcast(I32), 0)
+        nc.gpsimd.memset(tab_sc[:].bitcast(I32), 0)
         w2_sc = tile([P, 2, N], U8, "w2_sc")
         nc.vector.memset(w2_sc[:].rearrange("p a n -> p (a n)").bitcast(I32), 0)
 
@@ -55,14 +55,14 @@ def tile_list_boolean_tree_retrieval_kernel(
                 raw[b, a, half][:], w1[512 * a : 512 * a + 512, c0 : c0 + 256].rearrange("(p j) c -> p j c", j=4)
             )
 
-        load_w1(0, 0, 0)
         for q in range(4):
-            nc.sync.dma_start(
+            nc.gpsimd.dma_start(
                 tab_sc[32 * q : 32 * q + 8, :].bitcast(I32), tab_scales[:, 4 * q : 4 * q + 4, :].bitcast(I32)
             )
         load_tab(0)
         gain_t = tile([P, 2, 4], F32, "gain_t")
         nc.sync.dma_start(gain_t[:], gain.rearrange("(b p t) -> p b t", b=2, t=4))
+        load_w1(0, 0, 0)
         load_w1(0, 0, 1)
         load_tab(1)
         load_w1(0, 1, 0)
@@ -108,9 +108,9 @@ def tile_list_boolean_tree_retrieval_kernel(
 
         banks = {}
 
-        def first_pass(b, t, a):
+        def first_pass(b, t, a, start):
             for s in range(2):
-                if a == 0:
+                if start:
                     banks[b, t, s] = ps.tile([P, BANK], F32, name="d%d%d%d" % (b, t, s), tag="bank%d" % (2 * t + s))
                 cols = slice(BANK * s, BANK * (s + 1))
                 nc.tensor.matmul_mx(
@@ -119,8 +119,8 @@ def tile_list_boolean_tree_retrieval_kernel(
                     lhsT_scale=w_sc[b, a][:, 128 * t : 128 * (t + 1)],
                     rhs=v_w[a][:, cols].bitcast(FP8X4),
                     rhs_scale=v_sc[4 * a : P, cols],
-                    start=(a == 0),
-                    stop=(a == 1),
+                    start=start,
+                    stop=not start,
                 )
 
         h = {}
@@ -137,7 +137,7 @@ def tile_list_boolean_tree_retrieval_kernel(
         quant_w1(0, 0, 0, 4)
         nc.vector.tensor_copy(v_w[1][:], tab_w[1][:].bitcast(U32).indirect(offs_t[:]))
         for t in range(4):
-            first_pass(0, t, 0)
+            first_pass(0, t, 0, True)
         cast_w1(0, 1, 0, False)
         cast_w1(0, 1, 1, False, 0, 24)
         cast_w1(0, 1, 1, True, 24, 64)
@@ -145,19 +145,17 @@ def tile_list_boolean_tree_retrieval_kernel(
         quant_w1(0, 1, 1, 2)
         quant_w1(0, 1, 2, 4)
         for t in range(4):
-            first_pass(0, t, 1)
+            first_pass(0, t, 1, False)
         cast_w1(1, 0, 0, True)
 
         z0 = tile([P, 4 * M], F32, "z0")
         z1a = tile([P, 4 * M], F32, "z1a")
         gain_first = tile([P, M], F32, "gain_first")
-        gain_last = tile([P, 256], F32, "gain_last", tag="z1bc")
         spread = [gain_first[:]] + [z0[:, M * u : M * (u + 1)] for u in range(4)]
-        spread = spread + [z1a[:, 0:M], z1a[:, M : 2 * M], z1a[:, 2 * M : 2 * M + 256]]
+        spread = spread + [z1a[:, 0:M], z1a[:, M : 2 * M], z1a[:, 2 * M : 3 * M]]
         for u in range(8):
             width = spread[u].shape[1]
             nc.scalar.copy(spread[u], gain_t[:, u // 4, u % 4 : u % 4 + 1].to_broadcast([P, width]))
-        nc.scalar.copy(gain_last[:], gain_t[:, 1, 3:4].to_broadcast([P, 256]))
 
         left = {}
 
@@ -193,10 +191,13 @@ def tile_list_boolean_tree_retrieval_kernel(
         gather_right(1, z0[:, M : 2 * M], 0, M)
         sigmoid_h(0, 3)
         quant_w1(1, 1, 0, 4)
-        for t in range(4):
-            first_pass(1, t, 0)
-        for t in range(4):
-            first_pass(1, t, 1)
+        for t in range(2):
+            first_pass(1, t, 0, True)
+        for t in range(2):
+            first_pass(1, t, 1, False)
+        for t in range(2, 4):
+            first_pass(1, t, 1, True)
+            first_pass(1, t, 0, False)
         gather_left(3, "w_bf11")
         gather_right(2, z0[:, 2 * M : 3 * M], 0, M)
         for t in range(4):
@@ -208,59 +209,69 @@ def tile_list_boolean_tree_retrieval_kernel(
         gather_right(4, z1a[:, 0:256], 0, 256)
         gather_left(6)
         gather_right(5, z1a[:, M : M + 256], 0, 256)
-        left[7] = tile([P, M], F32, "left7")
-        nc.vector.tensor_tensor(left[7][:, 0:256], h[1, 3][:].indirect(pos1_t[:, 0:16]), spread[7], MULT)
+        gather_left(7)
         gather_right(6, z1a[:, 2 * M : 2 * M + 256], 0, 256)
-        nc.vector.tensor_tensor(left[7][:, 256:512], h[1, 3][:].indirect(pos1_t[:, 16:32]), gain_last[:], MULT)
         gather_right(7, z1a[:, 3 * M : 3 * M + 256], 0, 256)
         weave("1a", z1a[:].rearrange("p (t m) -> p t m", t=4)[:, :, 0:256], 256)
-        z1bc = tile([P, 2 * M], F32, "z1bc")
-        for c in range(2):
-            for t in range(4):
-                o = M * c + 128 * t
-                gather_right(4 + t, z1bc[:, o : o + 128], 256 + 128 * c, 384 + 128 * c)
-            weave("1" + "bc"[c], z1bc[:, M * c : M * (c + 1)].rearrange("p (t m) -> p t m", t=4), 128)
-
-        z_code = [tile([P, M], U32, "z_code0", tag="left4"), tile([P, M], U32, "z_code1")]
+        z_code = [tile([P, M], U32, "z_code%d" % a) for a in range(2)]
         z_sc = [tile([P, M], U8, "z_sc%d" % a) for a in range(2)]
 
         def quant_z(a, name, m0, m1):
             nc.vector.quantize_mx(z_code[a][:, m0:m1].bitcast(FP8X4), z_sc[a][:, m0:m1], z_bf[name][:])
 
         quant_z(0, "0", 0, M)
+        z1bc = tile([P, 2 * M], F32, "z1bc", tag="zbf0")
+        for c in range(2):
+            part = z1bc[:, M * c : M * (c + 1)]
+            for t in range(4):
+                gather_right(4 + t, part[:, 128 * t : 128 * (t + 1)], 256 + 128 * c, 384 + 128 * c)
+            weave("1" + "bc"[c], part.rearrange("p (t m) -> p t m", t=4), 128)
         quant_z(1, "1a", 0, 256)
         quant_z(1, "1b", 256, 384)
         quant_z(1, "1c", 384, 512)
 
-        def second_pass(bank, n, a, m0, m1, stop):
+        def second_pass(bank, n, a, m0, m1, start, stop):
             nc.tensor.matmul_mx(
                 bank[:, m0:m1],
                 lhsT=w2_w[:, a, 256 * n : 256 * (n + 1)].bitcast(FP4X4),
                 lhsT_scale=w2_sc[:, a, 128 * n : 128 * (n + 1)],
                 rhs=z_code[a][:, m0:m1].bitcast(FP8X4),
                 rhs_scale=z_sc[a][:, m0:m1],
-                start=(a == 0),
+                start=start,
                 stop=stop,
             )
 
-        y, not_y, right = {}, {}, {}
+        e, y, not_y, right = {}, {}, {}, {}
         for n in range(4):
-            bank = ps.tile([P, BANK], F32, name="e%d" % n, tag="bank%d" % n)
-            second_pass(bank, n, 0, 0, M, False)
+            e[n] = ps.tile([P, BANK], F32, name="e%d" % n, tag="bank%d" % n)
+        e_late = ps.tile([P, BANK], F32, name="e_late", tag="bank4")
+        for c in range(3):
+            second_pass(e[0], 0, 0, 128 * c, 128 * (c + 1), c == 0, False)
+        second_pass(e_late, 0, 0, 384, 512, True, False)
+        for n in range(1, 4):
+            second_pass(e[n], n, 0, 0, M, True, False)
+        for c in range(3):
+            second_pass(e[0], 0, 1, 128 * c, 128 * (c + 1), False, c == 2)
+        second_pass(e_late, 0, 1, 384, 512, False, True)
+        for n in range(1, 4):
+            second_pass(e[n], n, 1, 0, M, False, True)
+
+        def sigmoid_e(dst, n, scale):
             if n == 0:
-                for c in range(4):
-                    second_pass(bank, n, 1, 128 * c, 128 * (c + 1), c == 3)
+                nc.scalar.activation(dst[:, 0:384], e[0][:, 0:384], SIGMOID, scale=scale)
+                nc.scalar.activation(dst[:, 384:512], e_late[:, 384:512], SIGMOID, scale=scale)
             else:
-                second_pass(bank, n, 1, 0, M, True)
-            not_y[n] = tile([P, M], F32, "not_y%d" % n)
-            y[n] = tile([P, M], F32, "y%d" % n)
-            nc.scalar.activation(not_y[n][:], bank[:], SIGMOID, scale=-1.0)
-            nc.scalar.activation(y[n][:], bank[:], SIGMOID)
+                nc.scalar.activation(dst[:], e[n][:], SIGMOID, scale=scale)
+
         for n in range(5):
             if n < 4:
+                not_y[n] = tile([P, M], F32, "not_y%d" % n)
+                sigmoid_e(not_y[n], n, -1.0)
                 right[n] = tile([P, J], F32, "right%d" % n)
                 nc.vector.tensor_copy(right[n][:], not_y[n][:].indirect(pos4_t[:]))
             if n > 0:
+                y[n - 1] = tile([P, M], F32, "y%d" % (n - 1))
+                sigmoid_e(y[n - 1], n - 1, 1.0)
                 res = tile([P, J], F32, "res%d" % (n - 1))
                 nc.vector.tensor_tensor(res[:], y[n - 1][:].indirect(pos3_t[:]), right[n - 1][:], MULT)
                 nc.sync.dma_start(out[P * (n - 1) : P * n, :], res[:])

@@ -36,7 +36,7 @@ def tile_list_boolean_tree_retrieval_kernel(
             return t
 
         tab_sc = tile([P, T], U8, "tab_sc")
-        nc.gpsimd.memset(tab_sc[:].bitcast(I32), 0)
+        nc.vector.memset(tab_sc[:].bitcast(I32), 0)
         w2_sc = tile([P, 2, N], U8, "w2_sc")
         nc.vector.memset(w2_sc[:].rearrange("p a n -> p (a n)").bitcast(I32), 0)
 
@@ -55,13 +55,13 @@ def tile_list_boolean_tree_retrieval_kernel(
                 raw[b, a, half][:], w1[512 * a : 512 * a + 512, c0 : c0 + 256].rearrange("(p j) c -> p j c", j=4)
             )
 
+        gain_t = tile([P, 2, 4], F32, "gain_t")
+        nc.sync.dma_start(gain_t[:], gain.rearrange("(b p t) -> p b t", b=2, t=4))
         for q in range(4):
-            nc.gpsimd.dma_start(
+            nc.sync.dma_start(
                 tab_sc[32 * q : 32 * q + 8, :].bitcast(I32), tab_scales[:, 4 * q : 4 * q + 4, :].bitcast(I32)
             )
         load_tab(0)
-        gain_t = tile([P, 2, 4], F32, "gain_t")
-        nc.sync.dma_start(gain_t[:], gain.rearrange("(b p t) -> p b t", b=2, t=4))
         load_w1(0, 0, 0)
         load_w1(0, 0, 1)
         load_tab(1)
@@ -92,8 +92,9 @@ def tile_list_boolean_tree_retrieval_kernel(
         w_sc = {(b, a): tile([P, 512], U8, "w_sc%d%d" % (b, a)) for b in range(2) for a in range(2)}
 
         def cast_w1(b, a, half, on_vector, m0=0, m1=64):
-            dst = w_bf[b, a][:].rearrange("p (t m j) -> p m j t", t=4, j=4)[:, 64 * half + m0 : 64 * half + m1]
-            src = raw[b, a, half][:].rearrange("p j (m t) -> p m j t", t=4)[:, m0:m1]
+            dst = w_bf[b, a][:].rearrange("p (u t m j) -> p u m j t", u=2, t=2, j=4)
+            dst = dst[:, :, 64 * half + m0 : 64 * half + m1]
+            src = raw[b, a, half][:].rearrange("p j (m u t) -> p u m j t", u=2, t=2)[:, :, m0:m1]
             if on_vector:
                 nc.vector.tensor_copy(dst, src)
             else:
@@ -133,7 +134,8 @@ def tile_list_boolean_tree_retrieval_kernel(
         nc.vector.tensor_copy(v_sc[:], tab_sc[:].indirect(offs_t[:]))
         nc.vector.tensor_copy(v_w[0][:], tab_w[0][:].bitcast(U32).indirect(offs_t[:]))
         cast_w1(0, 0, 0, False)
-        cast_w1(0, 0, 1, False)
+        cast_w1(0, 0, 1, False, 0, 24)
+        cast_w1(0, 0, 1, True, 24, 64)
         quant_w1(0, 0, 0, 4)
         nc.vector.tensor_copy(v_w[1][:], tab_w[1][:].bitcast(U32).indirect(offs_t[:]))
         for t in range(4):

@@ -14,8 +14,10 @@ MULT = mybir.AluOpType.mult
 SIGMOID = mybir.ActivationFunctionType.Sigmoid
 
 P = 128
+HALF = 64
 K, T, S, H, M, N, J = 1024, 2048, 1024, 1024, 512, 512, 256
 BANK = 512
+FIRST, SMALL = 256, 128
 FLOPS = 2 * K * H * S + 2 * H * N * M
 
 
@@ -40,38 +42,37 @@ def tile_list_boolean_tree_retrieval_kernel(
         w2_sc = tile([P, 2, N], U8, "w2_sc")
         nc.vector.memset(w2_sc[:].rearrange("p a n -> p (a n)").bitcast(I32), 0)
 
-        offs_t = load_list(offs, "offs_t")
-
         tab_w = [tile([P, T], I32, "tab_w%d" % a) for a in range(2)]
         raw = {}
 
         def load_tab(a):
             nc.sync.dma_start(tab_w[a][:], tab_words[a].rearrange("p t i -> p (t i)").bitcast(I32))
 
-        def load_w1(b, a, half):
-            raw[b, a, half] = tile([P, 4, 256], F32, "raw%d%d%d" % (b, a, half))
-            c0 = 512 * b + 256 * half
-            nc.sync.dma_start(
-                raw[b, a, half][:], w1[512 * a : 512 * a + 512, c0 : c0 + 256].rearrange("(p j) c -> p j c", j=4)
-            )
+        def load_w1(name, a, c0, c1):
+            raw[name, a] = tile([P, 4, c1 - c0], F32, "raw%s%d" % (name, a))
+            nc.sync.dma_start(raw[name, a][:], w1[512 * a : 512 * a + 512, c0:c1].rearrange("(p j) c -> p j c", j=4))
 
-        gain_t = tile([P, 2, 4], F32, "gain_t")
-        nc.sync.dma_start(gain_t[:], gain.rearrange("(b p t) -> p b t", b=2, t=4))
+        offs_t = load_list(offs, "offs_t")
+        gain_lo = tile([P, 2, 8], F32, "gain_lo")
+        first_gains = gain[0:512].rearrange("(q p t) -> p q t", q=2, t=4)
+        for half in range(2):
+            nc.sync.dma_start(gain_lo[HALF * half : HALF * (half + 1), :, 0:3], first_gains[:, :, half : half + 3])
         for q in range(4):
             nc.sync.dma_start(
                 tab_sc[32 * q : 32 * q + 8, :].bitcast(I32), tab_scales[:, 4 * q : 4 * q + 4, :].bitcast(I32)
             )
         load_tab(0)
-        load_w1(0, 0, 0)
-        load_w1(0, 0, 1)
+        load_w1("q0", 0, 0, 256)
+        gain_hi = tile([P, 4], F32, "gain_hi")
+        nc.sync.dma_start(gain_hi[:], gain[512:1024].rearrange("(p t) -> p t", t=4))
         load_tab(1)
-        load_w1(0, 1, 0)
-        load_w1(0, 1, 1)
+        load_w1("q0", 1, 0, 256)
+        load_w1("q1", 0, 256, 512)
         pos1_t = load_list(pos1, "pos1_t")
         pos2_t = load_list(pos2, "pos2_t")
-        for a in range(2):
-            for half in range(2):
-                load_w1(1, a, half)
+        load_w1("q1", 1, 256, 512)
+        load_w1("hi", 0, 512, 1024)
+        load_w1("hi", 1, 512, 1024)
         w2_w = tile([P, 2, 2 * N], U8, "w2_w")
         nc.sync.dma_start(w2_w[:].bitcast(I32), w2_words.rearrange("a p c -> p a c").bitcast(I32))
         for q in range(4):
@@ -83,41 +84,50 @@ def tile_list_boolean_tree_retrieval_kernel(
         pos4_t = load_list(pos4, "pos4_t")
 
         warm = tile([P, 1], F32, "warm")
-        nc.scalar.activation(warm[:], gain_t[:, 0, 0:1], SIGMOID)
+        nc.scalar.activation(warm[:], gain_lo[:, 0, 0:1], SIGMOID)
 
         v_sc = tile([P, S], U8, "v_sc")
         v_w = [tile([P, S], U32, "v_w%d" % a) for a in range(2)]
-        w_bf = {(b, a): tile([P, 2048], BF16, "w_bf%d%d" % (b, a)) for b in range(2) for a in range(2)}
-        w_code = {(b, a): tile([P, 512], U32, "w_code%d%d" % (b, a)) for b in range(2) for a in range(2)}
-        w_sc = {(b, a): tile([P, 512], U8, "w_sc%d%d" % (b, a)) for b in range(2) for a in range(2)}
+        w_bf, w_code, w_sc = {}, {}, {}
 
-        def cast_w1(b, a, half, on_vector, m0=0, m1=64):
-            dst = w_bf[b, a][:].rearrange("p (u t m j) -> p u m j t", u=2, t=2, j=4)
-            dst = dst[:, :, 64 * half + m0 : 64 * half + m1]
-            src = raw[b, a, half][:].rearrange("p j (m u t) -> p u m j t", u=2, t=2)[:, :, m0:m1]
+        def gather_words(a, j0, j1):
+            nc.vector.tensor_copy(v_w[a][:, j0:j1], tab_w[a][:].bitcast(U32).indirect(offs_t[:, j0 // 16 : j1 // 16]))
+
+        def round_w1(name, a, u, on_vector=False):
+            width = raw[name, a].shape[2]
+            src = raw[name, a][:].rearrange("p j (m u t) -> p u m j t", u=2, t=2)
+            if u is None:
+                w_bf[name, a, u] = tile([P, 4 * width], BF16, "w_bf%s%d" % (name, a))
+                dst = w_bf[name, a, u][:].rearrange("p (u t m j) -> p u m j t", u=2, t=2, j=4)
+            else:
+                w_bf[name, a, u] = tile([P, 2 * width], BF16, "w_bf%s%d%d" % (name, a, u))
+                dst = w_bf[name, a, u][:].rearrange("p (t m j) -> p m j t", t=2, j=4)
+                src = src[:, u]
             if on_vector:
                 nc.vector.tensor_copy(dst, src)
             else:
                 nc.scalar.copy(dst, src)
 
-        def quant_w1(b, a, t0, t1):
-            nc.vector.quantize_mx(
-                w_code[b, a][:, 128 * t0 : 128 * t1].bitcast(FP8X4),
-                w_sc[b, a][:, 128 * t0 : 128 * t1],
-                w_bf[b, a][:, 512 * t0 : 512 * t1],
-            )
+        def quant_w1(name, a, u, first_tile):
+            words = w_bf[name, a, u].shape[1] // 4
+            code = tile([P, words], U32, "w_code%d%d" % (first_tile, a))
+            scale = tile([P, words], U8, "w_sc%d%d" % (first_tile, a))
+            nc.vector.quantize_mx(code[:].bitcast(FP8X4), scale[:], w_bf[name, a, u][:])
+            for i in range(words // P):
+                w_code[first_tile + i, a] = code[:, P * i : P * (i + 1)]
+                w_sc[first_tile + i, a] = scale[:, P * i : P * (i + 1)]
 
         banks = {}
 
-        def first_pass(b, t, a, start):
+        def first_pass(u, a, start):
             for s in range(2):
                 if start:
-                    banks[b, t, s] = ps.tile([P, BANK], F32, name="d%d%d%d" % (b, t, s), tag="bank%d" % (2 * t + s))
+                    banks[u, s] = ps.tile([P, BANK], F32, name="d%d%d" % (u, s), tag="bank%d" % (2 * (u % 4) + s))
                 cols = slice(BANK * s, BANK * (s + 1))
                 nc.tensor.matmul_mx(
-                    banks[b, t, s][:],
-                    lhsT=w_code[b, a][:, 128 * t : 128 * (t + 1)].bitcast(FP8X4),
-                    lhsT_scale=w_sc[b, a][:, 128 * t : 128 * (t + 1)],
+                    banks[u, s][:],
+                    lhsT=w_code[u, a].bitcast(FP8X4),
+                    lhsT_scale=w_sc[u, a],
                     rhs=v_w[a][:, cols].bitcast(FP8X4),
                     rhs_scale=v_sc[4 * a : P, cols],
                     start=start,
@@ -126,49 +136,58 @@ def tile_list_boolean_tree_retrieval_kernel(
 
         h = {}
 
-        def sigmoid_h(b, t):
-            h[b, t] = tile([P, S], F32, "h%d%d" % (b, t))
+        def sigmoid_h(u):
+            h[u] = tile([P, S], F32, "h%d" % u)
             for s in range(2):
-                nc.scalar.activation(h[b, t][:, BANK * s : BANK * (s + 1)], banks[b, t, s][:], SIGMOID)
-
-        nc.vector.tensor_copy(v_sc[:], tab_sc[:].indirect(offs_t[:]))
-        nc.vector.tensor_copy(v_w[0][:], tab_w[0][:].bitcast(U32).indirect(offs_t[:]))
-        cast_w1(0, 0, 0, False)
-        cast_w1(0, 0, 1, False, 0, 24)
-        cast_w1(0, 0, 1, True, 24, 64)
-        quant_w1(0, 0, 0, 4)
-        nc.vector.tensor_copy(v_w[1][:], tab_w[1][:].bitcast(U32).indirect(offs_t[:]))
-        for t in range(4):
-            first_pass(0, t, 0, True)
-        cast_w1(0, 1, 0, False)
-        cast_w1(0, 1, 1, False, 0, 24)
-        cast_w1(0, 1, 1, True, 24, 64)
-        quant_w1(0, 1, 0, 1)
-        quant_w1(0, 1, 1, 2)
-        quant_w1(0, 1, 2, 4)
-        for t in range(4):
-            first_pass(0, t, 1, False)
-        cast_w1(1, 0, 0, True)
+                nc.scalar.activation(h[u][:, BANK * s : BANK * (s + 1)], banks[u, s][:], SIGMOID)
 
         z0 = tile([P, 4 * M], F32, "z0")
         z1a = tile([P, 4 * M], F32, "z1a")
         gain_first = tile([P, M], F32, "gain_first")
-        spread = [gain_first[:]] + [z0[:, M * u : M * (u + 1)] for u in range(4)]
-        spread = spread + [z1a[:, 0:M], z1a[:, M : 2 * M], z1a[:, 2 * M : 3 * M]]
-        for u in range(8):
-            width = spread[u].shape[1]
-            nc.scalar.copy(spread[u], gain_t[:, u // 4, u % 4 : u % 4 + 1].to_broadcast([P, width]))
+        gain_fifth = tile([P, M], F32, "gain_fifth")
+        stage2 = tile([P, M], F32, "stage2")
+        spread = [gain_first[:], z0[:, 0:M], z0[:, 2 * M : 3 * M], stage2[:], gain_fifth[:]]
+        spread = spread + [z1a[:, M * t : M * (t + 1)] for t in range(3)]
+
+        def spread_gain(u):
+            col = gain_lo[:, u // 2, 2 * (u % 2) : 2 * (u % 2) + 1] if u < 4 else gain_hi[:, u - 4 : u - 3]
+            nc.scalar.copy(spread[u], col.to_broadcast([P, M]))
+
+        nc.vector.tensor_copy(v_sc[:], tab_sc[:].indirect(offs_t[:]))
+        gather_words(0, 0, S)
+        for u in range(4):
+            spread_gain(u)
+        round_w1("q0", 0, None)
+        quant_w1("q0", 0, None, 0)
+        gather_words(1, 0, BANK)
+        gather_words(1, BANK, S)
+        for u in range(2):
+            first_pass(u, 0, True)
+        for u in range(4, 8):
+            spread_gain(u)
+        for u in range(2):
+            round_w1("q0", 1, u)
+        for u in range(2):
+            quant_w1("q0", 1, u, u)
+            first_pass(u, 1, False)
+        for a in range(2):
+            round_w1("q1", a, None, True)
+            quant_w1("q1", a, None, 2)
+        for u in range(2, 4):
+            first_pass(u, 0, True)
+            first_pass(u, 1, False)
 
         left = {}
 
         def gather_left(u, tag=None):
             left[u] = tile([P, M], F32, "left%d" % u, tag=tag)
-            nc.vector.tensor_tensor(left[u][:], h[u // 4, u % 4][:].indirect(pos1_t[:]), spread[u], MULT)
+            nc.vector.tensor_tensor(left[u][:], h[u][:].indirect(pos1_t[:]), spread[u], MULT)
 
         def gather_right(u, dst, m0, m1):
-            nc.vector.tensor_tensor(
-                dst, h[u // 4, u % 4][:].indirect(pos2_t[:, m0 // 16 : m1 // 16]), left[u][:, m0:m1], MULT
-            )
+            nc.vector.tensor_tensor(dst, h[u][:].indirect(pos2_t[:, m0 // 16 : m1 // 16]), left[u][:, m0:m1], MULT)
+
+        def plane(t):
+            return z0[:, M * t : M * (t + 1)]
 
         z_bf = {}
 
@@ -179,42 +198,56 @@ def tile_list_boolean_tree_retrieval_kernel(
                 planes.rearrange("p t (c i) -> p c t i", i=4),
             )
 
-        sigmoid_h(0, 0)
-        sigmoid_h(0, 1)
-        gather_left(0)
-        gather_left(1)
-        cast_w1(1, 0, 1, False)
-        gather_right(0, z0[:, 0:M], 0, M)
-        sigmoid_h(0, 2)
-        quant_w1(1, 0, 0, 4)
-        gather_left(2, "w_bf10")
-        cast_w1(1, 1, 0, False)
-        cast_w1(1, 1, 1, False)
-        gather_right(1, z0[:, M : 2 * M], 0, M)
-        sigmoid_h(0, 3)
-        quant_w1(1, 1, 0, 4)
-        for t in range(2):
-            first_pass(1, t, 0, True)
-        for t in range(2):
-            first_pass(1, t, 1, False)
-        for t in range(2, 4):
-            first_pass(1, t, 1, True)
-            first_pass(1, t, 0, False)
-        gather_left(3, "w_bf11")
-        gather_right(2, z0[:, 2 * M : 3 * M], 0, M)
-        for t in range(4):
-            sigmoid_h(1, t)
-        gather_left(4)
-        gather_right(3, z0[:, 3 * M : 4 * M], 0, M)
-        weave("0", z0[:].rearrange("p (t m) -> p t m", t=4), M)
+        def move_first(t):
+            nc.sync.dma_start(plane(t + 1)[0:HALF, :], plane(t)[HALF:P, :])
+
+        def move_second(t, src):
+            nc.sync.dma_start(plane(t)[HALF:P, :], src[0:HALF, :])
+            nc.sync.dma_start(plane(t + 1)[HALF:P, :], src[HALF:P, :])
+
+        sigmoid_h(0)
+        sigmoid_h(1)
+        gather_left(0, "w_bfq11")
+        gather_left(1, "gain_first")
+        gather_right(0, plane(0), 0, M)
+        move_first(0)
+        sigmoid_h(2)
+        round_w1("hi", 0, 0)
+        quant_w1("hi", 0, 0, 4)
+        gather_left(2, "w_bfhi00")
+        gather_right(1, plane(2), 0, M)
+        move_first(2)
+        sigmoid_h(3)
+        round_w1("hi", 1, 0)
+        quant_w1("hi", 1, 0, 4)
+        gather_left(3, "w_bfhi10")
+        for u in range(4, 6):
+            first_pass(u, 0, True)
+            first_pass(u, 1, False)
+        gather_right(2, stage2[:], 0, M)
+        move_second(0, stage2)
+        round_w1("hi", 0, 1)
+        round_w1("hi", 1, 1)
+        quant_w1("hi", 0, 1, 6)
+        stage3 = tile([P, M], F32, "stage3", tag="w_bfhi01")
+        gather_right(3, stage3[:], 0, M)
+        move_second(2, stage3)
+        quant_w1("hi", 1, 1, 6)
+        for u in range(6, 8):
+            first_pass(u, 0, True)
+            first_pass(u, 1, False)
+        for u in range(4, 8):
+            sigmoid_h(u)
+        gather_left(4, "w_bfhi11")
         gather_left(5)
-        gather_right(4, z1a[:, 0:256], 0, 256)
+        gather_right(4, z1a[:, 0:FIRST], 0, FIRST)
+        weave("0", z0[:].rearrange("p (t m) -> p t m", t=4), M)
         gather_left(6)
-        gather_right(5, z1a[:, M : M + 256], 0, 256)
+        gather_right(5, z1a[:, M : M + FIRST], 0, FIRST)
         gather_left(7)
-        gather_right(6, z1a[:, 2 * M : 2 * M + 256], 0, 256)
-        gather_right(7, z1a[:, 3 * M : 3 * M + 256], 0, 256)
-        weave("1a", z1a[:].rearrange("p (t m) -> p t m", t=4)[:, :, 0:256], 256)
+        gather_right(6, z1a[:, 2 * M : 2 * M + FIRST], 0, FIRST)
+        gather_right(7, z1a[:, 3 * M : 3 * M + FIRST], 0, FIRST)
+        weave("1a", z1a[:].rearrange("p (t m) -> p t m", t=4)[:, :, 0:FIRST], FIRST)
         z_code = [tile([P, M], U32, "z_code%d" % a) for a in range(2)]
         z_sc = [tile([P, M], U8, "z_sc%d" % a) for a in range(2)]
 
@@ -225,12 +258,13 @@ def tile_list_boolean_tree_retrieval_kernel(
         z1bc = tile([P, 2 * M], F32, "z1bc", tag="zbf0")
         for c in range(2):
             part = z1bc[:, M * c : M * (c + 1)]
+            m0 = FIRST + SMALL * c
             for t in range(4):
-                gather_right(4 + t, part[:, 128 * t : 128 * (t + 1)], 256 + 128 * c, 384 + 128 * c)
-            weave("1" + "bc"[c], part.rearrange("p (t m) -> p t m", t=4), 128)
-        quant_z(1, "1a", 0, 256)
-        quant_z(1, "1b", 256, 384)
-        quant_z(1, "1c", 384, 512)
+                gather_right(4 + t, part[:, SMALL * t : SMALL * (t + 1)], m0, m0 + SMALL)
+            weave("1" + "bc"[c], part.rearrange("p (t m) -> p t m", t=4), SMALL)
+        quant_z(1, "1a", 0, FIRST)
+        quant_z(1, "1b", FIRST, FIRST + SMALL)
+        quant_z(1, "1c", FIRST + SMALL, M)
 
         def second_pass(bank, n, a, m0, m1, start, stop):
             nc.tensor.matmul_mx(

@@ -53,10 +53,10 @@ def tile_list_boolean_tree_retrieval_kernel(
             nc.sync.dma_start(raw[name, a][:], w1[512 * a : 512 * a + 512, c0:c1].rearrange("(p j) c -> p j c", j=4))
 
         offs_t = load_list(offs, "offs_t")
-        gain_lo = tile([P, 2, 8], F32, "gain_lo")
-        first_gains = gain[0:512].rearrange("(q p t) -> p q t", q=2, t=4)
+        gain_lo = tile([P, 2, 4], F32, "gain_lo")
         for half in range(2):
-            nc.sync.dma_start(gain_lo[HALF * half : HALF * (half + 1), :, 0:3], first_gains[:, :, half : half + 3])
+            shifted = gain[half : 512 + half].rearrange("(q p t) -> p q t", q=2, t=4)
+            nc.sync.dma_start(gain_lo[HALF * half : HALF * (half + 1), :, :], shifted)
         for q in range(4):
             nc.sync.dma_start(
                 tab_sc[32 * q : 32 * q + 8, :].bitcast(I32), tab_scales[:, 4 * q : 4 * q + 4, :].bitcast(I32)
@@ -68,9 +68,9 @@ def tile_list_boolean_tree_retrieval_kernel(
         load_tab(1)
         load_w1("q0", 1, 0, 256)
         load_w1("q1", 0, 256, 512)
+        load_w1("q1", 1, 256, 512)
         pos1_t = load_list(pos1, "pos1_t")
         pos2_t = load_list(pos2, "pos2_t")
-        load_w1("q1", 1, 256, 512)
         load_w1("hi", 0, 512, 1024)
         load_w1("hi", 1, 512, 1024)
         w2_w = tile([P, 2, 2 * N], U8, "w2_w")
@@ -93,14 +93,14 @@ def tile_list_boolean_tree_retrieval_kernel(
         def gather_words(a, j0, j1):
             nc.vector.tensor_copy(v_w[a][:, j0:j1], tab_w[a][:].bitcast(U32).indirect(offs_t[:, j0 // 16 : j1 // 16]))
 
-        def round_w1(name, a, u, on_vector=False):
+        def round_w1(name, a, u, on_vector=False, tag=None):
             width = raw[name, a].shape[2]
             src = raw[name, a][:].rearrange("p j (m u t) -> p u m j t", u=2, t=2)
             if u is None:
-                w_bf[name, a, u] = tile([P, 4 * width], BF16, "w_bf%s%d" % (name, a))
+                w_bf[name, a, u] = tile([P, 4 * width], BF16, "w_bf%s%d" % (name, a), tag=tag)
                 dst = w_bf[name, a, u][:].rearrange("p (u t m j) -> p u m j t", u=2, t=2, j=4)
             else:
-                w_bf[name, a, u] = tile([P, 2 * width], BF16, "w_bf%s%d%d" % (name, a, u))
+                w_bf[name, a, u] = tile([P, 2 * width], BF16, "w_bf%s%d%d" % (name, a, u), tag=tag)
                 dst = w_bf[name, a, u][:].rearrange("p (t m j) -> p m j t", t=2, j=4)
                 src = src[:, u]
             if on_vector:
@@ -122,7 +122,7 @@ def tile_list_boolean_tree_retrieval_kernel(
         def first_pass(u, a, start):
             for s in range(2):
                 if start:
-                    banks[u, s] = ps.tile([P, BANK], F32, name="d%d%d" % (u, s), tag="bank%d" % (2 * (u % 4) + s))
+                    banks[u, s] = ps.tile([P, BANK], F32, name="d%d%d" % (u, s), tag="bank%d" % (2 * (u if u < 4 else u % 2) + s))
                 cols = slice(BANK * s, BANK * (s + 1))
                 nc.tensor.matmul_mx(
                     banks[u, s][:],
@@ -144,9 +144,10 @@ def tile_list_boolean_tree_retrieval_kernel(
         z0 = tile([P, 4 * M], F32, "z0")
         z1a = tile([P, 4 * M], F32, "z1a")
         gain_first = tile([P, M], F32, "gain_first")
+        gain_third = tile([P, M], F32, "gain_third")
         gain_fifth = tile([P, M], F32, "gain_fifth")
         stage2 = tile([P, M], F32, "stage2")
-        spread = [gain_first[:], z0[:, 0:M], z0[:, 2 * M : 3 * M], stage2[:], gain_fifth[:]]
+        spread = [gain_first[:], z0[:, 0:M], gain_third[:], stage2[:], gain_fifth[:]]
         spread = spread + [z1a[:, M * t : M * (t + 1)] for t in range(3)]
 
         def spread_gain(u):
@@ -170,12 +171,10 @@ def tile_list_boolean_tree_retrieval_kernel(
         for u in range(2):
             quant_w1("q0", 1, u, u)
             first_pass(u, 1, False)
-        for a in range(2):
-            round_w1("q1", a, None, True)
-            quant_w1("q1", a, None, 2)
+        round_w1("q1", 0, None, True)
+        quant_w1("q1", 0, None, 2)
         for u in range(2, 4):
             first_pass(u, 0, True)
-            first_pass(u, 1, False)
 
         left = {}
 
@@ -191,8 +190,8 @@ def tile_list_boolean_tree_retrieval_kernel(
 
         z_bf = {}
 
-        def weave(name, planes, width):
-            z_bf[name] = tile([P, 4 * width], BF16, "zbf" + name)
+        def weave(name, planes, width, tag=None):
+            z_bf[name] = tile([P, 4 * width], BF16, "zbf" + name, tag=tag)
             nc.scalar.copy(
                 z_bf[name][:].rearrange("p (c i t) -> p c t i", i=4, t=4),
                 planes.rearrange("p t (c i) -> p c t i", i=4),
@@ -205,49 +204,55 @@ def tile_list_boolean_tree_retrieval_kernel(
             nc.sync.dma_start(plane(t)[HALF:P, :], src[0:HALF, :])
             nc.sync.dma_start(plane(t + 1)[HALF:P, :], src[HALF:P, :])
 
+        round_w1("q1", 1, None, True)
+        quant_w1("q1", 1, None, 2)
+        for u in range(2, 4):
+            first_pass(u, 1, False)
         sigmoid_h(0)
         sigmoid_h(1)
         gather_left(0, "w_bfq11")
         gather_left(1, "gain_first")
         gather_right(0, plane(0), 0, M)
         move_first(0)
-        sigmoid_h(2)
-        round_w1("hi", 0, 0)
-        quant_w1("hi", 0, 0, 4)
-        gather_left(2, "w_bfhi00")
         gather_right(1, plane(2), 0, M)
         move_first(2)
-        sigmoid_h(3)
-        round_w1("hi", 1, 0)
-        quant_w1("hi", 1, 0, 4)
-        gather_left(3, "w_bfhi10")
+        round_w1("hi", 0, 0)
+        quant_w1("hi", 0, 0, 4)
         for u in range(4, 6):
             first_pass(u, 0, True)
+        sigmoid_h(2)
+        round_w1("hi", 1, 0, tag="w_code21")
+        sigmoid_h(3)
+        round_w1("hi", 0, 1, tag="w_sc21")
+        gather_left(2, "w_bfhi00")
+        quant_w1("hi", 1, 0, 4)
+        for u in range(4, 6):
             first_pass(u, 1, False)
+        gather_left(3, "w_code21")
         gather_right(2, stage2[:], 0, M)
         move_second(0, stage2)
-        round_w1("hi", 0, 1)
-        round_w1("hi", 1, 1)
         quant_w1("hi", 0, 1, 6)
-        stage3 = tile([P, M], F32, "stage3", tag="w_bfhi01")
+        stage3 = tile([P, M], F32, "stage3", tag="w_sc21")
         gather_right(3, stage3[:], 0, M)
         move_second(2, stage3)
+        sigmoid_h(4)
+        round_w1("hi", 1, 1, tag="w_code41")
         quant_w1("hi", 1, 1, 6)
+        sigmoid_h(5)
         for u in range(6, 8):
             first_pass(u, 0, True)
             first_pass(u, 1, False)
-        for u in range(4, 8):
             sigmoid_h(u)
-        gather_left(4, "w_bfhi11")
+        gather_left(4, "w_code41")
         gather_left(5)
         gather_right(4, z1a[:, 0:FIRST], 0, FIRST)
-        weave("0", z0[:].rearrange("p (t m) -> p t m", t=4), M)
+        weave("0", z0[:].rearrange("p (t m) -> p t m", t=4), M, "w_code61")
         gather_left(6)
         gather_right(5, z1a[:, M : M + FIRST], 0, FIRST)
         gather_left(7)
         gather_right(6, z1a[:, 2 * M : 2 * M + FIRST], 0, FIRST)
         gather_right(7, z1a[:, 3 * M : 3 * M + FIRST], 0, FIRST)
-        weave("1a", z1a[:].rearrange("p (t m) -> p t m", t=4)[:, :, 0:FIRST], FIRST)
+        weave("1a", z1a[:].rearrange("p (t m) -> p t m", t=4)[:, :, 0:FIRST], FIRST, "z0")
         z_code = [tile([P, M], U32, "z_code%d" % a) for a in range(2)]
         z_sc = [tile([P, M], U8, "z_sc%d" % a) for a in range(2)]
 
@@ -255,7 +260,7 @@ def tile_list_boolean_tree_retrieval_kernel(
             nc.vector.quantize_mx(z_code[a][:, m0:m1].bitcast(FP8X4), z_sc[a][:, m0:m1], z_bf[name][:])
 
         quant_z(0, "0", 0, M)
-        z1bc = tile([P, 2 * M], F32, "z1bc", tag="zbf0")
+        z1bc = tile([P, 2 * M], F32, "z1bc", tag="w_code61")
         for c in range(2):
             part = z1bc[:, M * c : M * (c + 1)]
             m0 = FIRST + SMALL * c
@@ -279,8 +284,8 @@ def tile_list_boolean_tree_retrieval_kernel(
 
         e, y, not_y, right = {}, {}, {}, {}
         for n in range(4):
-            e[n] = ps.tile([P, BANK], F32, name="e%d" % n, tag="bank%d" % n)
-        e_late = ps.tile([P, BANK], F32, name="e_late", tag="bank4")
+            e[n] = ps.tile([P, BANK], F32, name="e%d" % n, tag="bank%d" % (4 + n))
+        e_late = ps.tile([P, BANK], F32, name="e_late", tag="bank0")
         for c in range(3):
             second_pass(e[0], 0, 0, 128 * c, 128 * (c + 1), c == 0, False)
         second_pass(e_late, 0, 0, 384, 512, True, False)

@@ -148,7 +148,8 @@ def tile_list_boolean_tree_retrieval_kernel(
         gain_fifth = tile([P, M], F32, "gain_fifth")
         stage2 = tile([P, M], F32, "stage2")
         spread = [gain_first[:], z0[:, 0:M], gain_third[:], stage2[:], gain_fifth[:]]
-        spread = spread + [z1a[:, M * t : M * (t + 1)] for t in range(3)]
+        gain_last = tile([P, M], F32, "gain_last")
+        spread = spread + [z1a[:, 0:M], z1a[:, M : 2 * M], gain_last[:]]
 
         def spread_gain(u):
             col = gain_lo[:, u // 2, 2 * (u % 2) : 2 * (u % 2) + 1] if u < 4 else gain_hi[:, u - 4 : u - 3]
@@ -232,34 +233,34 @@ def tile_list_boolean_tree_retrieval_kernel(
         gather_right(2, stage2[:], 0, M)
         move_second(0, stage2)
         quant_w1("hi", 0, 1, 6)
-        stage3 = tile([P, M], F32, "stage3", tag="w_sc21")
+        round_w1("hi", 1, 1)
+        quant_w1("hi", 1, 1, 6)
+        stage3 = tile([P, M], F32, "stage3", tag="w_bfhi11")
         gather_right(3, stage3[:], 0, M)
         move_second(2, stage3)
         sigmoid_h(4)
-        round_w1("hi", 1, 1, tag="w_code41")
-        quant_w1("hi", 1, 1, 6)
         sigmoid_h(5)
         for u in range(6, 8):
             first_pass(u, 0, True)
             first_pass(u, 1, False)
             sigmoid_h(u)
-        gather_left(4, "w_code41")
+        gather_left(4)
         gather_left(5)
         gather_right(4, z1a[:, 0:FIRST], 0, FIRST)
         weave("0", z0[:].rearrange("p (t m) -> p t m", t=4), M, "w_code61")
         gather_left(6)
         gather_right(5, z1a[:, M : M + FIRST], 0, FIRST)
-        gather_left(7)
         gather_right(6, z1a[:, 2 * M : 2 * M + FIRST], 0, FIRST)
-        gather_right(7, z1a[:, 3 * M : 3 * M + FIRST], 0, FIRST)
-        weave("1a", z1a[:].rearrange("p (t m) -> p t m", t=4)[:, :, 0:FIRST], FIRST, "z0")
-        z_code = [tile([P, M], U32, "z_code%d" % a) for a in range(2)]
+        gather_left(7)
+        z_code = [tile([P, M], U32, "z_code0", tag="gain_last"), tile([P, M], U32, "z_code1")]
         z_sc = [tile([P, M], U8, "z_sc%d" % a) for a in range(2)]
 
         def quant_z(a, name, m0, m1):
             nc.vector.quantize_mx(z_code[a][:, m0:m1].bitcast(FP8X4), z_sc[a][:, m0:m1], z_bf[name][:])
 
         quant_z(0, "0", 0, M)
+        gather_right(7, z1a[:, 3 * M : 3 * M + FIRST], 0, FIRST)
+        weave("1a", z1a[:].rearrange("p (t m) -> p t m", t=4)[:, :, 0:FIRST], FIRST, "z0")
         z1bc = tile([P, 2 * M], F32, "z1bc", tag="w_code61")
         for c in range(2):
             part = z1bc[:, M * c : M * (c + 1)]

@@ -17,7 +17,7 @@ P = 128
 HALF = 64
 K, T, S, H, M, N, J = 1024, 2048, 1024, 1024, 512, 512, 256
 BANK = 512
-FIRST, SMALL = 256, 128
+FIRST, SMALL, LAST = 256, 128, 64
 FLOPS = 2 * K * H * S + 2 * H * N * M
 
 
@@ -142,14 +142,7 @@ def tile_list_boolean_tree_retrieval_kernel(
                 nc.scalar.activation(h[u][:, BANK * s : BANK * (s + 1)], banks[u, s][:], SIGMOID)
 
         z0 = tile([P, 4 * M], F32, "z0")
-        z1a = tile([P, 4 * M], F32, "z1a")
-        gain_first = tile([P, M], F32, "gain_first")
-        gain_third = tile([P, M], F32, "gain_third")
-        gain_fifth = tile([P, M], F32, "gain_fifth")
-        stage2 = tile([P, M], F32, "stage2")
-        spread = [gain_first[:], z0[:, 0:M], gain_third[:], stage2[:], gain_fifth[:]]
-        gain_last = tile([P, M], F32, "gain_last")
-        spread = spread + [z1a[:, 0:M], z1a[:, M : 2 * M], gain_last[:]]
+        spread = [tile([P, M], F32, "gain_row%d" % u)[:] for u in range(8)]
 
         def spread_gain(u):
             col = gain_lo[:, u // 2, 2 * (u % 2) : 2 * (u % 2) + 1] if u < 4 else gain_hi[:, u - 4 : u - 3]
@@ -169,19 +162,22 @@ def tile_list_boolean_tree_retrieval_kernel(
             spread_gain(u)
         for u in range(2):
             round_w1("q0", 1, u)
-        for u in range(2):
-            quant_w1("q0", 1, u, u)
-            first_pass(u, 1, False)
+        quant_w1("q0", 1, 0, 0)
+        first_pass(0, 1, False)
         round_w1("q1", 0, None, True)
+        quant_w1("q0", 1, 1, 1)
+        first_pass(1, 1, False)
         quant_w1("q1", 0, None, 2)
         for u in range(2, 4):
             first_pass(u, 0, True)
 
         left = {}
 
-        def gather_left(u, tag=None):
-            left[u] = tile([P, M], F32, "left%d" % u, tag=tag)
-            nc.vector.tensor_tensor(left[u][:], h[u][:].indirect(pos1_t[:]), spread[u], MULT)
+        def gather_left(u, m0=0, m1=M):
+            if u not in left:
+                left[u] = tile([P, M], F32, "left%d" % u)
+            picked = h[u][:].indirect(pos1_t[:, m0 // 16 : m1 // 16])
+            nc.vector.tensor_tensor(left[u][:, m0:m1], picked, spread[u][:, m0:m1], MULT)
 
         def gather_right(u, dst, m0, m1):
             nc.vector.tensor_tensor(dst, h[u][:].indirect(pos2_t[:, m0 // 16 : m1 // 16]), left[u][:, m0:m1], MULT)
@@ -191,10 +187,10 @@ def tile_list_boolean_tree_retrieval_kernel(
 
         z_bf = {}
 
-        def weave(name, planes, width, tag=None):
-            z_bf[name] = tile([P, 4 * width], BF16, "zbf" + name, tag=tag)
+        def weave(name, planes, dst):
+            z_bf[name] = dst
             nc.scalar.copy(
-                z_bf[name][:].rearrange("p (c i t) -> p c t i", i=4, t=4),
+                dst.rearrange("p (c i t) -> p c t i", i=4, t=4),
                 planes.rearrange("p t (c i) -> p c t i", i=4),
             )
 
@@ -206,68 +202,74 @@ def tile_list_boolean_tree_retrieval_kernel(
             nc.sync.dma_start(plane(t + 1)[HALF:P, :], src[HALF:P, :])
 
         round_w1("q1", 1, None, True)
+        sigmoid_h(0)
+        sigmoid_h(1)
+        gather_left(0)
         quant_w1("q1", 1, None, 2)
         for u in range(2, 4):
             first_pass(u, 1, False)
-        sigmoid_h(0)
-        sigmoid_h(1)
-        gather_left(0, "w_bfq11")
-        gather_left(1, "gain_first")
+        gather_left(1)
         gather_right(0, plane(0), 0, M)
         move_first(0)
         gather_right(1, plane(2), 0, M)
         move_first(2)
         round_w1("hi", 0, 0)
         quant_w1("hi", 0, 0, 4)
-        for u in range(4, 6):
-            first_pass(u, 0, True)
+        first_pass(4, 0, True)
         sigmoid_h(2)
         round_w1("hi", 1, 0, tag="w_code21")
         sigmoid_h(3)
-        round_w1("hi", 0, 1, tag="w_sc21")
-        gather_left(2, "w_bfhi00")
-        quant_w1("hi", 1, 0, 4)
-        for u in range(4, 6):
-            first_pass(u, 1, False)
-        gather_left(3, "w_code21")
-        gather_right(2, stage2[:], 0, M)
-        move_second(0, stage2)
-        quant_w1("hi", 0, 1, 6)
         round_w1("hi", 1, 1)
+        gather_left(2)
+        gather_left(3)
+        quant_w1("hi", 1, 0, 4)
+        first_pass(4, 1, False)
+        first_pass(5, 1, True)
+        first_pass(5, 0, False)
+        round_w1("hi", 0, 1, tag="w_code21")
         quant_w1("hi", 1, 1, 6)
-        stage3 = tile([P, M], F32, "stage3", tag="w_bfhi11")
-        gather_right(3, stage3[:], 0, M)
-        move_second(2, stage3)
+        stage = tile([P, 2, M], F32, "stage", tag="rawhi1")
+        for i in range(2):
+            gather_right(2 + i, stage[:, i, :], 0, M)
+            move_second(2 * i, stage[:, i, :])
+        quant_w1("hi", 0, 1, 6)
         sigmoid_h(4)
         sigmoid_h(5)
         for u in range(6, 8):
             first_pass(u, 0, True)
             first_pass(u, 1, False)
             sigmoid_h(u)
-        gather_left(4)
-        gather_left(5)
-        gather_right(4, z1a[:, 0:FIRST], 0, FIRST)
-        weave("0", z0[:].rearrange("p (t m) -> p t m", t=4), M, "w_code61")
-        gather_left(6)
-        gather_right(5, z1a[:, M : M + FIRST], 0, FIRST)
-        gather_right(6, z1a[:, 2 * M : 2 * M + FIRST], 0, FIRST)
-        gather_left(7)
-        z_code = [tile([P, M], U32, "z_code0", tag="gain_last"), tile([P, M], U32, "z_code1")]
+        for u in range(4, 7):
+            gather_left(u)
+        z1a = tile([P, 4, FIRST], F32, "z1a", tag="w_sc61")
+        for t in range(3):
+            gather_right(4 + t, z1a[:, t, :], 0, FIRST)
+        weave("0", z0[:].rearrange("p (t m) -> p t m", t=4), tile([P, 4 * M], BF16, "z_bf0", tag="w_code61")[:])
+        gather_left(7, 0, FIRST)
+        gather_left(7, FIRST, M)
+        gather_right(7, z1a[:, 3, :], 0, FIRST)
+        late = tile([P, 4 * M], F32, "late", tag="z0")
+        weave("1a", z1a[:], late[:, 0 : 2 * FIRST].bitcast(BF16))
+        z_code = [tile([P, M], U32, "z_code%d" % a) for a in range(2)]
         z_sc = [tile([P, M], U8, "z_sc%d" % a) for a in range(2)]
 
         def quant_z(a, name, m0, m1):
-            nc.vector.quantize_mx(z_code[a][:, m0:m1].bitcast(FP8X4), z_sc[a][:, m0:m1], z_bf[name][:])
+            nc.vector.quantize_mx(z_code[a][:, m0:m1].bitcast(FP8X4), z_sc[a][:, m0:m1], z_bf[name])
 
-        quant_z(0, "0", 0, M)
-        gather_right(7, z1a[:, 3 * M : 3 * M + FIRST], 0, FIRST)
-        weave("1a", z1a[:].rearrange("p (t m) -> p t m", t=4)[:, :, 0:FIRST], FIRST, "z0")
-        z1bc = tile([P, 2 * M], F32, "z1bc", tag="w_code61")
-        for c in range(2):
-            part = z1bc[:, M * c : M * (c + 1)]
-            m0 = FIRST + SMALL * c
+        z_bf1 = tile([P, 4 * (M - FIRST)], BF16, "z_bf1")
+
+        def late_part(m0, m1):
+            part = late[:, 4 * m0 : 4 * m1].rearrange("p (t m) -> p t m", t=4)
             for t in range(4):
-                gather_right(4 + t, part[:, SMALL * t : SMALL * (t + 1)], m0, m0 + SMALL)
-            weave("1" + "bc"[c], part.rearrange("p (t m) -> p t m", t=4), SMALL)
+                gather_right(4 + t, part[:, t, :], m0, m1)
+            weave("late", part, z_bf1[:, 4 * (m0 - FIRST) : 4 * (m1 - FIRST)])
+
+        late_part(FIRST, FIRST + SMALL)
+        quant_z(0, "0", 0, M)
+        late_part(M - 2 * LAST, M - LAST)
+        late_part(M - LAST, M)
+        z_bf["1b"] = z_bf1[:, 0 : 4 * SMALL]
+        z_bf["1c"] = z_bf1[:, 4 * SMALL : 8 * SMALL]
         quant_z(1, "1a", 0, FIRST)
         quant_z(1, "1b", FIRST, FIRST + SMALL)
         quant_z(1, "1c", FIRST + SMALL, M)

@@ -38,7 +38,8 @@ def tile_list_boolean_tree_retrieval_kernel(
             return t
 
         tab_sc = tile([P, T], U8, "tab_sc")
-        nc.vector.memset(tab_sc[:].bitcast(I32), 0)
+        nc.vector.memset(tab_sc[:, 0 : T // 2].bitcast(I32), 0)
+        nc.gpsimd.memset(tab_sc[:, T // 2 : T].bitcast(I32), 0)
         w2_sc = tile([P, 2, N], U8, "w2_sc")
         nc.vector.memset(w2_sc[:].rearrange("p a n -> p (a n)").bitcast(I32), 0)
 
@@ -154,8 +155,7 @@ def tile_list_boolean_tree_retrieval_kernel(
             spread_gain(u)
         round_w1("q0", 0, None)
         quant_w1("q0", 0, None, 0)
-        gather_words(1, 0, BANK)
-        gather_words(1, BANK, S)
+        gather_words(1, 0, S)
         for u in range(2):
             first_pass(u, 0, True)
         for u in range(4, 8):
@@ -264,8 +264,8 @@ def tile_list_boolean_tree_retrieval_kernel(
                 gather_right(4 + t, part[:, t, :], m0, m1)
             weave("late", part, z_bf1[:, 4 * (m0 - FIRST) : 4 * (m1 - FIRST)])
 
-        late_part(FIRST, FIRST + SMALL)
         quant_z(0, "0", 0, M)
+        late_part(FIRST, FIRST + SMALL)
         late_part(M - 2 * LAST, M - LAST)
         late_part(M - LAST, M)
         z_bf["1b"] = z_bf1[:, 0 : 4 * SMALL]
@@ -317,5 +317,7 @@ def tile_list_boolean_tree_retrieval_kernel(
                 y[n - 1] = tile([P, M], F32, "y%d" % (n - 1))
                 sigmoid_e(y[n - 1], n - 1, 1.0)
                 res = tile([P, J], F32, "res%d" % (n - 1))
-                nc.vector.tensor_tensor(res[:], y[n - 1][:].indirect(pos3_t[:]), right[n - 1][:], MULT)
-                nc.sync.dma_start(out[P * (n - 1) : P * n, :], res[:])
+                for j0, j1 in [(0, J)] if n < 4 else [(0, J // 2), (J // 2, J)]:
+                    picked = y[n - 1][:].indirect(pos3_t[:, j0 // 16 : j1 // 16])
+                    nc.vector.tensor_tensor(res[:, j0:j1], picked, right[n - 1][:, j0:j1], MULT)
+                    nc.sync.dma_start(out[P * (n - 1) : P * n, j0:j1], res[:, j0:j1])

@@ -38,8 +38,7 @@ def tile_list_boolean_tree_retrieval_kernel(
             return t
 
         tab_sc = tile([P, T], U8, "tab_sc")
-        nc.vector.memset(tab_sc[:, 0 : T // 2].bitcast(I32), 0)
-        nc.gpsimd.memset(tab_sc[:, T // 2 : T].bitcast(I32), 0)
+        nc.vector.memset(tab_sc[:].bitcast(I32), 0)
         w2_sc = tile([P, 2, N], U8, "w2_sc")
         nc.vector.memset(w2_sc[:].rearrange("p a n -> p (a n)").bitcast(I32), 0)
 

@@ -108,6 +108,14 @@ def tile_list_boolean_tree_retrieval_kernel(
             else:
                 nc.scalar.copy(dst, src)
 
+        def share_round(name, a):
+            width = raw[name, a].shape[2]
+            w_bf[name, a, None] = tile([P, 4 * width], BF16, "w_bf%s%d" % (name, a))
+            src = raw[name, a][:].rearrange("p j (m u t) -> p u m j t", u=2, t=2)
+            dst = w_bf[name, a, None][:].rearrange("p (u t m j) -> p u m j t", u=2, t=2, j=4)
+            nc.scalar.copy(dst[:, 0], src[:, 0])
+            nc.vector.tensor_copy(dst[:, 1], src[:, 1])
+
         def quant_w1(name, a, u, first_tile):
             words = w_bf[name, a, u].shape[1] // 4
             code = tile([P, words], U32, "w_code%d%d" % (first_tile, a))
@@ -163,7 +171,7 @@ def tile_list_boolean_tree_retrieval_kernel(
             round_w1("q0", 1, u)
         quant_w1("q0", 1, 0, 0)
         first_pass(0, 1, False)
-        round_w1("q1", 0, None, True)
+        share_round("q1", 0)
         quant_w1("q0", 1, 1, 1)
         first_pass(1, 1, False)
         quant_w1("q1", 0, None, 2)

@@ -15,6 +15,7 @@ SIGMOID = mybir.ActivationFunctionType.Sigmoid
 
 P = 128
 HALF = 64
+ROWS = 96
 K, T, S, H, M, N, J = 1024, 2048, 1024, 1024, 512, 512, 256
 BANK = 512
 FIRST, SMALL, LAST = 256, 128, 64
@@ -38,7 +39,9 @@ def tile_list_boolean_tree_retrieval_kernel(
             return t
 
         tab_sc = tile([P, T], U8, "tab_sc")
-        nc.vector.memset(tab_sc[:].bitcast(I32), 0)
+        nc.vector.memset(tab_sc[0:ROWS, :].bitcast(I32), 0)
+        v_sc = tile([P, S], U8, "v_sc")
+        nc.vector.memset(v_sc[:].bitcast(I32), 0)
         w2_sc = tile([P, 2, N], U8, "w2_sc")
         nc.vector.memset(w2_sc[:].rearrange("p a n -> p (a n)").bitcast(I32), 0)
 
@@ -52,15 +55,14 @@ def tile_list_boolean_tree_retrieval_kernel(
             raw[name, a] = tile([P, 4, c1 - c0], F32, "raw%s%d" % (name, a))
             nc.sync.dma_start(raw[name, a][:], w1[512 * a : 512 * a + 512, c0:c1].rearrange("(p j) c -> p j c", j=4))
 
-        offs_t = load_list(offs, "offs_t")
         gain_lo = tile([P, 2, 4], F32, "gain_lo")
         for half in range(2):
             shifted = gain[half : 512 + half].rearrange("(q p t) -> p q t", q=2, t=4)
-            nc.sync.dma_start(gain_lo[HALF * half : HALF * (half + 1), :, :], shifted)
-        for q in range(4):
-            nc.sync.dma_start(
-                tab_sc[32 * q : 32 * q + 8, :].bitcast(I32), tab_scales[:, 4 * q : 4 * q + 4, :].bitcast(I32)
-            )
+            nc.scalar.dma_start(gain_lo[HALF * half : HALF * (half + 1), :, :], shifted)
+        scale_rows = tab_scales.rearrange("a (q r) t -> r q a t", r=4)
+        for r in range(4):
+            nc.sync.dma_start(tab_sc[ROWS + r : P : 4, :].bitcast(I32), scale_rows[r].bitcast(I32))
+        offs_t = load_list(offs, "offs_t")
         load_tab(0)
         load_w1("q0", 0, 0, 256)
         gain_hi = tile([P, 4], F32, "gain_hi")
@@ -83,10 +85,11 @@ def tile_list_boolean_tree_retrieval_kernel(
         pos3_t = load_list(pos3, "pos3_t")
         pos4_t = load_list(pos4, "pos4_t")
 
-        warm = tile([P, 1], F32, "warm")
-        nc.scalar.activation(warm[:], gain_lo[:, 0, 0:1], SIGMOID)
+        warm = tile([P, 2], F32, "warm")
+        nc.gpsimd.memset(warm[:, 0:1], 0.0)
+        nc.scalar.activation(warm[:, 1:2], warm[:, 0:1], SIGMOID)
 
-        v_sc = tile([P, S], U8, "v_sc")
+        picked_sc = tile([P, S], U8, "picked_sc")
         v_w = [tile([P, S], U32, "v_w%d" % a) for a in range(2)]
         w_bf, w_code, w_sc = {}, {}, {}
 
@@ -156,15 +159,18 @@ def tile_list_boolean_tree_retrieval_kernel(
             col = gain_lo[:, u // 2, 2 * (u % 2) : 2 * (u % 2) + 1] if u < 4 else gain_hi[:, u - 4 : u - 3]
             nc.scalar.copy(spread[u], col.to_broadcast([P, M]))
 
-        nc.vector.tensor_copy(v_sc[:], tab_sc[:].indirect(offs_t[:]))
+        nc.vector.tensor_copy(picked_sc[:], tab_sc[:].indirect(offs_t[:]))
+        for q in range(4):
+            nc.scalar.dma_start(
+                v_sc[32 * q : 32 * q + 8, :].bitcast(I32), picked_sc[ROWS + 8 * q : ROWS + 8 * q + 8, :].bitcast(I32)
+            )
         gather_words(0, 0, S)
         for u in range(4):
             spread_gain(u)
         round_w1("q0", 0, None)
         quant_w1("q0", 0, None, 0)
         gather_words(1, 0, S)
-        for u in range(2):
-            first_pass(u, 0, True)
+        first_pass(0, 0, True)
         for u in range(4, 8):
             spread_gain(u)
         for u in range(2):
@@ -173,7 +179,8 @@ def tile_list_boolean_tree_retrieval_kernel(
         first_pass(0, 1, False)
         share_round("q1", 0)
         quant_w1("q0", 1, 1, 1)
-        first_pass(1, 1, False)
+        first_pass(1, 1, True)
+        first_pass(1, 0, False)
         quant_w1("q1", 0, None, 2)
         for u in range(2, 4):
             first_pass(u, 0, True)

@@ -91,7 +91,7 @@ def tile_list_boolean_tree_retrieval_kernel(
 
         picked_sc = tile([P, S], U8, "picked_sc")
         v_w = [tile([P, S], U32, "v_w%d" % a) for a in range(2)]
-        w_bf, w_code, w_sc = {}, {}, {}
+        w_bf, w_code, w_sc, whole = {}, {}, {}, {}
 
         def gather_words(a, j0, j1):
             nc.vector.tensor_copy(v_w[a][:, j0:j1], tab_w[a][:].bitcast(U32).indirect(offs_t[:, j0 // 16 : j1 // 16]))
@@ -111,19 +111,12 @@ def tile_list_boolean_tree_retrieval_kernel(
             else:
                 nc.scalar.copy(dst, src)
 
-        def share_round(name, a):
-            width = raw[name, a].shape[2]
-            w_bf[name, a, None] = tile([P, 4 * width], BF16, "w_bf%s%d" % (name, a))
-            src = raw[name, a][:].rearrange("p j (m u t) -> p u m j t", u=2, t=2)
-            dst = w_bf[name, a, None][:].rearrange("p (u t m j) -> p u m j t", u=2, t=2, j=4)
-            nc.scalar.copy(dst[:, 0], src[:, 0])
-            nc.vector.tensor_copy(dst[:, 1], src[:, 1])
-
         def quant_w1(name, a, u, first_tile):
             words = w_bf[name, a, u].shape[1] // 4
             code = tile([P, words], U32, "w_code%d%d" % (first_tile, a))
             scale = tile([P, words], U8, "w_sc%d%d" % (first_tile, a))
             nc.vector.quantize_mx(code[:].bitcast(FP8X4), scale[:], w_bf[name, a, u][:])
+            whole[first_tile, a] = (code, scale)
             for i in range(words // P):
                 w_code[first_tile + i, a] = code[:, P * i : P * (i + 1)]
                 w_sc[first_tile + i, a] = scale[:, P * i : P * (i + 1)]
@@ -170,6 +163,17 @@ def tile_list_boolean_tree_retrieval_kernel(
         round_w1("q0", 0, None)
         quant_w1("q0", 0, None, 0)
         gather_words(1, 0, S)
+        idle = ps.tile([P, BANK], F32, name="idle", tag="bank7")
+        for i in range(5):
+            nc.tensor.matmul_mx(
+                idle[:, 0 : 2 * P],
+                lhsT=w_code[0, 0].bitcast(FP8X4),
+                lhsT_scale=w_sc[0, 0],
+                rhs=whole[0, 0][0][:].bitcast(FP8X4),
+                rhs_scale=whole[0, 0][1][:],
+                start=i == 0,
+                stop=i == 4,
+            )
         first_pass(0, 0, True)
         for u in range(4, 8):
             spread_gain(u)
@@ -177,10 +181,11 @@ def tile_list_boolean_tree_retrieval_kernel(
             round_w1("q0", 1, u)
         quant_w1("q0", 1, 0, 0)
         first_pass(0, 1, False)
-        share_round("q1", 0)
+        round_w1("q1", 0, None, True)
         quant_w1("q0", 1, 1, 1)
         first_pass(1, 1, True)
         first_pass(1, 0, False)
+        round_w1("q1", 1, 0, True)
         quant_w1("q1", 0, None, 2)
         for u in range(2, 4):
             first_pass(u, 0, True)
@@ -215,16 +220,17 @@ def tile_list_boolean_tree_retrieval_kernel(
             nc.sync.dma_start(plane(t)[HALF:P, :], src[0:HALF, :])
             nc.sync.dma_start(plane(t + 1)[HALF:P, :], src[HALF:P, :])
 
-        round_w1("q1", 1, None, True)
         sigmoid_h(0)
+        round_w1("q1", 1, 1)
         sigmoid_h(1)
         gather_left(0)
-        quant_w1("q1", 1, None, 2)
-        for u in range(2, 4):
-            first_pass(u, 1, False)
-        gather_left(1)
+        quant_w1("q1", 1, 0, 2)
+        first_pass(2, 1, False)
         gather_right(0, plane(0), 0, M)
         move_first(0)
+        quant_w1("q1", 1, 1, 3)
+        first_pass(3, 1, False)
+        gather_left(1)
         gather_right(1, plane(2), 0, M)
         move_first(2)
         round_w1("hi", 0, 0)

@@ -91,7 +91,7 @@ def tile_list_boolean_tree_retrieval_kernel(
 
         picked_sc = tile([P, S], U8, "picked_sc")
         v_w = [tile([P, S], U32, "v_w%d" % a) for a in range(2)]
-        w_bf, w_code, w_sc, whole = {}, {}, {}, {}
+        w_bf, w_code, w_sc = {}, {}, {}
 
         def gather_words(a, j0, j1):
             nc.vector.tensor_copy(v_w[a][:, j0:j1], tab_w[a][:].bitcast(U32).indirect(offs_t[:, j0 // 16 : j1 // 16]))
@@ -116,7 +116,6 @@ def tile_list_boolean_tree_retrieval_kernel(
             code = tile([P, words], U32, "w_code%d%d" % (first_tile, a))
             scale = tile([P, words], U8, "w_sc%d%d" % (first_tile, a))
             nc.vector.quantize_mx(code[:].bitcast(FP8X4), scale[:], w_bf[name, a, u][:])
-            whole[first_tile, a] = (code, scale)
             for i in range(words // P):
                 w_code[first_tile + i, a] = code[:, P * i : P * (i + 1)]
                 w_sc[first_tile + i, a] = scale[:, P * i : P * (i + 1)]
@@ -163,17 +162,6 @@ def tile_list_boolean_tree_retrieval_kernel(
         round_w1("q0", 0, None)
         quant_w1("q0", 0, None, 0)
         gather_words(1, 0, S)
-        idle = ps.tile([P, BANK], F32, name="idle", tag="bank7")
-        for i in range(5):
-            nc.tensor.matmul_mx(
-                idle[:, 0 : 2 * P],
-                lhsT=w_code[0, 0].bitcast(FP8X4),
-                lhsT_scale=w_sc[0, 0],
-                rhs=whole[0, 0][0][:].bitcast(FP8X4),
-                rhs_scale=whole[0, 0][1][:],
-                start=i == 0,
-                stop=i == 4,
-            )
         first_pass(0, 0, True)
         for u in range(4, 8):
             spread_gain(u)

@@ -12,13 +12,14 @@ FP8X4 = mybir.dt.float8_e4m3fn_x4
 FP4X4 = mybir.dt.float4_e2m1fn_x4
 MULT = mybir.AluOpType.mult
 SIGMOID = mybir.ActivationFunctionType.Sigmoid
+COPY = mybir.ActivationFunctionType.Copy
 
 P = 128
 HALF = 64
 ROWS = 96
 K, T, S, H, M, N, J = 1024, 2048, 1024, 1024, 512, 512, 256
 BANK = 512
-FIRST, SMALL, LAST = 256, 128, 64
+PARTS = ((0, 320), (320, 448), (448, 512))
 FLOPS = 2 * K * H * S + 2 * H * N * M
 
 
@@ -192,15 +193,6 @@ def tile_list_boolean_tree_retrieval_kernel(
         def plane(t):
             return z0[:, M * t : M * (t + 1)]
 
-        z_bf = {}
-
-        def weave(name, planes, dst):
-            z_bf[name] = dst
-            nc.scalar.copy(
-                dst.rearrange("p (c i t) -> p c t i", i=4, t=4),
-                planes.rearrange("p t (c i) -> p c t i", i=4),
-            )
-
         def move_first(t):
             nc.sync.dma_start(plane(t + 1)[0:HALF, :], plane(t)[HALF:P, :])
 
@@ -247,40 +239,43 @@ def tile_list_boolean_tree_retrieval_kernel(
             first_pass(u, 0, True)
             first_pass(u, 1, False)
             sigmoid_h(u)
-        for u in range(4, 7):
-            gather_left(u)
-        z1a = tile([P, 4, FIRST], F32, "z1a", tag="w_sc61")
-        for t in range(3):
-            gather_right(4 + t, z1a[:, t, :], 0, FIRST)
-        weave("0", z0[:].rearrange("p (t m) -> p t m", t=4), tile([P, 4 * M], BF16, "z_bf0", tag="w_code61")[:])
-        gather_left(7, 0, FIRST)
-        gather_left(7, FIRST, M)
-        gather_right(7, z1a[:, 3, :], 0, FIRST)
-        late = tile([P, 4 * M], F32, "late", tag="z0")
-        weave("1a", z1a[:], late[:, 0 : 2 * FIRST].bitcast(BF16))
         z_code = [tile([P, M], U32, "z_code%d" % a) for a in range(2)]
         z_sc = [tile([P, M], U8, "z_sc%d" % a) for a in range(2)]
 
-        def quant_z(a, name, m0, m1):
-            nc.vector.quantize_mx(z_code[a][:, m0:m1].bitcast(FP8X4), z_sc[a][:, m0:m1], z_bf[name])
+        def quant_z(a, src, m0, m1):
+            nc.vector.quantize_mx(z_code[a][:, m0:m1].bitcast(FP8X4), z_sc[a][:, m0:m1], src[:, 4 * m0 : 4 * m1])
 
-        z_bf1 = tile([P, 4 * (M - FIRST)], BF16, "z_bf1")
+        gather_left(4)
+        gather_left(5)
+        front = tile([P, 2, M], F32, "front", tag="w_sc61")
+        for t in range(2):
+            gather_right(4 + t, front[:, t, :], 0, M)
+        z_bf0 = tile([P, 4 * M], BF16, "z_bf0", tag="w_code61")
+        nc.scalar.copy(
+            z_bf0[:].rearrange("p (c i t) -> p c t i", i=4, t=4),
+            z0[:].rearrange("p (t c i) -> p c t i", t=4, i=4),
+        )
+        gather_left(6)
+        gather_left(7)
+        late = tile([P, 4 * M], F32, "late", tag="z0")
+        z_bf1 = late[:, 0 : 2 * M].bitcast(BF16)
 
-        def late_part(m0, m1):
-            part = late[:, 4 * m0 : 4 * m1].rearrange("p (t m) -> p t m", t=4)
-            for t in range(4):
-                gather_right(4 + t, part[:, t, :], m0, m1)
-            weave("late", part, z_bf1[:, 4 * (m0 - FIRST) : 4 * (m1 - FIRST)])
+        def weave_pair(u, planes, m0, m1):
+            dst = z_bf1[:, 4 * m0 : 4 * m1].rearrange("p (m u t) -> p u m t", u=2, t=2)
+            nc.scalar.copy(dst[:, u], planes.rearrange("p t m -> p m t"))
 
-        quant_z(0, "0", 0, M)
-        late_part(FIRST, FIRST + SMALL)
-        late_part(M - 2 * LAST, M - LAST)
-        late_part(M - LAST, M)
-        z_bf["1b"] = z_bf1[:, 0 : 4 * SMALL]
-        z_bf["1c"] = z_bf1[:, 4 * SMALL : 8 * SMALL]
-        quant_z(1, "1a", 0, FIRST)
-        quant_z(1, "1b", FIRST, FIRST + SMALL)
-        quant_z(1, "1c", FIRST + SMALL, M)
+        weave_pair(0, front[:], 0, M)
+        for i, (m0, m1) in enumerate(PARTS):
+            if i == 0:
+                quant_z(0, z_bf0[:], 0, 256)
+            part = late[:, 2 * (M + m0) : 2 * (M + m1)].rearrange("p (t m) -> p t m", t=2)
+            for t in range(2):
+                gather_right(6 + t, part[:, t, :], m0, m1)
+                if (i, t) == (1, 0):
+                    quant_z(0, z_bf0[:], 256, M)
+            weave_pair(1, part, m0, m1)
+        for m0, m1 in ((0, 256), (256, 384), (384, 512)):
+            quant_z(1, z_bf1, m0, m1)
 
         def second_pass(bank, n, a, m0, m1, start, stop):
             nc.tensor.matmul_mx(
@@ -293,39 +288,43 @@ def tile_list_boolean_tree_retrieval_kernel(
                 stop=stop,
             )
 
-        e, y, not_y, right = {}, {}, {}, {}
+        e, y, right = {}, {}, {}
         for n in range(4):
             e[n] = ps.tile([P, BANK], F32, name="e%d" % n, tag="bank%d" % (4 + n))
         e_late = ps.tile([P, BANK], F32, name="e_late", tag="bank0")
-        for c in range(3):
-            second_pass(e[0], 0, 0, 128 * c, 128 * (c + 1), c == 0, False)
-        second_pass(e_late, 0, 0, 384, 512, True, False)
+        for n in range(4):
+            second_pass(e[n], n, 0, 0, 256, True, False)
+        second_pass(e_late, 0, 0, 256, M, True, False)
         for n in range(1, 4):
-            second_pass(e[n], n, 0, 0, M, True, False)
-        for c in range(3):
-            second_pass(e[0], 0, 1, 128 * c, 128 * (c + 1), False, c == 2)
+            second_pass(e[n], n, 0, 256, M, False, False)
+        second_pass(e[0], 0, 1, 0, 256, False, True)
+        second_pass(e_late, 0, 1, 256, 384, False, False)
         second_pass(e_late, 0, 1, 384, 512, False, True)
         for n in range(1, 4):
             second_pass(e[n], n, 1, 0, M, False, True)
 
-        def sigmoid_e(dst, n, scale):
+        def pick_right(n):
+            y[n] = tile([P, M], F32, "y%d" % n)
             if n == 0:
-                nc.scalar.activation(dst[:, 0:384], e[0][:, 0:384], SIGMOID, scale=scale)
-                nc.scalar.activation(dst[:, 384:512], e_late[:, 384:512], SIGMOID, scale=scale)
+                nc.scalar.activation(y[0][:, 0:256], e[0][:, 0:256], SIGMOID)
+                nc.scalar.activation(y[0][:, 256:M], e_late[:, 256:M], SIGMOID)
             else:
-                nc.scalar.activation(dst[:], e[n][:], SIGMOID, scale=scale)
+                nc.scalar.activation(y[n][:], e[n][:], SIGMOID)
+            right[n] = tile([P, J], F32, "right%d" % n)
+            nc.vector.tensor_copy(right[n][:], y[n][:].indirect(pos4_t[:]))
 
-        for n in range(5):
-            if n < 4:
-                not_y[n] = tile([P, M], F32, "not_y%d" % n)
-                sigmoid_e(not_y[n], n, -1.0)
-                right[n] = tile([P, J], F32, "right%d" % n)
-                nc.vector.tensor_copy(right[n][:], not_y[n][:].indirect(pos4_t[:]))
-            if n > 0:
-                y[n - 1] = tile([P, M], F32, "y%d" % (n - 1))
-                sigmoid_e(y[n - 1], n - 1, 1.0)
-                res = tile([P, J], F32, "res%d" % (n - 1))
-                for j0, j1 in [(0, J)] if n < 4 else [(0, J // 2), (J // 2, J)]:
-                    picked = y[n - 1][:].indirect(pos3_t[:, j0 // 16 : j1 // 16])
-                    nc.vector.tensor_tensor(res[:, j0:j1], picked, right[n - 1][:, j0:j1], MULT)
-                    nc.sync.dma_start(out[P * (n - 1) : P * n, j0:j1], res[:, j0:j1])
+        def finish(n):
+            not_right = tile([P, J], F32, "not_right%d" % n)
+            nc.scalar.activation(not_right[:], right[n][:], COPY, bias=1.0, scale=-1.0)
+            res = tile([P, J], F32, "res%d" % n)
+            for j0, j1 in [(0, J)] if n < 3 else [(0, J // 2), (J // 2, J)]:
+                picked = y[n][:].indirect(pos3_t[:, j0 // 16 : j1 // 16])
+                nc.vector.tensor_tensor(res[:, j0:j1], picked, not_right[:, j0:j1], MULT)
+                nc.sync.dma_start(out[P * n : P * (n + 1), j0:j1], res[:, j0:j1])
+
+        for n in range(3):
+            pick_right(n)
+        finish(0)
+        pick_right(3)
+        for n in range(1, 4):
+            finish(n)

@@ -16,7 +16,6 @@ COPY = mybir.ActivationFunctionType.Copy
 
 P = 128
 HALF = 64
-ROWS = 96
 K, T, S, H, M, N, J = 1024, 2048, 1024, 1024, 512, 512, 256
 BANK = 512
 PARTS = ((0, 320), (320, 448), (448, 512))
@@ -40,7 +39,8 @@ def tile_list_boolean_tree_retrieval_kernel(
             return t
 
         tab_sc = tile([P, T], U8, "tab_sc")
-        nc.vector.memset(tab_sc[0:ROWS, :].bitcast(I32), 0)
+        nc.vector.memset(tab_sc[32:64, :].bitcast(I32), 0)
+        nc.vector.memset(tab_sc[64:P, :].bitcast(I32), 0)
         v_sc = tile([P, S], U8, "v_sc")
         nc.vector.memset(v_sc[:].bitcast(I32), 0)
         w2_sc = tile([P, 2, N], U8, "w2_sc")
@@ -62,17 +62,17 @@ def tile_list_boolean_tree_retrieval_kernel(
             nc.scalar.dma_start(gain_lo[HALF * half : HALF * (half + 1), :, :], shifted)
         scale_rows = tab_scales.rearrange("a (q r) t -> r q a t", r=4)
         for r in range(4):
-            nc.sync.dma_start(tab_sc[ROWS + r : P : 4, :].bitcast(I32), scale_rows[r].bitcast(I32))
+            nc.sync.dma_start(tab_sc[r:32:4, :].bitcast(I32), scale_rows[r].bitcast(I32))
         offs_t = load_list(offs, "offs_t")
         load_tab(0)
         load_w1("q0", 0, 0, 256)
         gain_hi = tile([P, 4], F32, "gain_hi")
         nc.sync.dma_start(gain_hi[:], gain[512:1024].rearrange("(p t) -> p t", t=4))
+        pos1_t = load_list(pos1, "pos1_t")
         load_tab(1)
         load_w1("q0", 1, 0, 256)
         load_w1("q1", 0, 256, 512)
         load_w1("q1", 1, 256, 512)
-        pos1_t = load_list(pos1, "pos1_t")
         pos2_t = load_list(pos2, "pos2_t")
         load_w1("hi", 0, 512, 1024)
         load_w1("hi", 1, 512, 1024)
@@ -153,10 +153,9 @@ def tile_list_boolean_tree_retrieval_kernel(
             nc.scalar.copy(spread[u], col.to_broadcast([P, M]))
 
         nc.vector.tensor_copy(picked_sc[:], tab_sc[:].indirect(offs_t[:]))
-        for q in range(4):
-            nc.scalar.dma_start(
-                v_sc[32 * q : 32 * q + 8, :].bitcast(I32), picked_sc[ROWS + 8 * q : ROWS + 8 * q + 8, :].bitcast(I32)
-            )
+        for q in range(1, 4):
+            nc.scalar.dma_start(v_sc[32 * q : 32 * q + 8, :].bitcast(I32), picked_sc[8 * q : 8 * q + 8, :].bitcast(I32))
+        nc.vector.tensor_copy(v_sc[0:8, :].bitcast(I32), picked_sc[0:8, :].bitcast(I32))
         gather_words(0, 0, S)
         for u in range(4):
             spread_gain(u)

@@ -11,6 +11,7 @@ U8 = mybir.dt.uint8
 FP8X4 = mybir.dt.float8_e4m3fn_x4
 FP4X4 = mybir.dt.float4_e2m1fn_x4
 MULT = mybir.AluOpType.mult
+SUBTRACT = mybir.AluOpType.subtract
 SIGMOID = mybir.ActivationFunctionType.Sigmoid
 COPY = mybir.ActivationFunctionType.Copy
 
@@ -18,7 +19,7 @@ P = 128
 HALF = 64
 K, T, S, H, M, N, J = 1024, 2048, 1024, 1024, 512, 512, 256
 BANK = 512
-PARTS = ((0, 320), (320, 448), (448, 512))
+PARTS = ((0, 192), (192, 320), (320, 448), (448, 512))
 FLOPS = 2 * K * H * S + 2 * H * N * M
 
 
@@ -45,6 +46,9 @@ def tile_list_boolean_tree_retrieval_kernel(
         nc.vector.memset(v_sc[:].bitcast(I32), 0)
         w2_sc = tile([P, 2, N], U8, "w2_sc")
         nc.vector.memset(w2_sc[:].rearrange("p a n -> p (a n)").bitcast(I32), 0)
+
+        ones = tile([P, J], F32, "ones")
+        nc.vector.memset(ones[:], 1.0)
 
         tab_w = [tile([P, T], I32, "tab_w%d" % a) for a in range(2)]
         raw = {}
@@ -264,16 +268,15 @@ def tile_list_boolean_tree_retrieval_kernel(
             nc.scalar.copy(dst[:, u], planes.rearrange("p t m -> p m t"))
 
         weave_pair(0, front[:], 0, M)
-        for i, (m0, m1) in enumerate(PARTS):
-            if i == 0:
-                quant_z(0, z_bf0[:], 0, 256)
+        quant_z(0, z_bf0[:], 0, 256)
+        for m0, m1 in PARTS:
             part = late[:, 2 * (M + m0) : 2 * (M + m1)].rearrange("p (t m) -> p t m", t=2)
             for t in range(2):
                 gather_right(6 + t, part[:, t, :], m0, m1)
-                if (i, t) == (1, 0):
-                    quant_z(0, z_bf0[:], 256, M)
             weave_pair(1, part, m0, m1)
-        for m0, m1 in ((0, 256), (256, 384), (384, 512)):
+        quant_z(1, z_bf1, 0, 256)
+        quant_z(0, z_bf0[:], 256, M)
+        for m0, m1 in ((256, 384), (384, 448), (448, 512)):
             quant_z(1, z_bf1, m0, m1)
 
         def second_pass(bank, n, a, m0, m1, start, stop):
@@ -287,43 +290,47 @@ def tile_list_boolean_tree_retrieval_kernel(
                 stop=stop,
             )
 
-        e, y, right = {}, {}, {}
-        for n in range(4):
-            e[n] = ps.tile([P, BANK], F32, name="e%d" % n, tag="bank%d" % (4 + n))
-        e_late = ps.tile([P, BANK], F32, name="e_late", tag="bank0")
-        for n in range(4):
+        first_ranges = ((0, 256), (256, 384), (384, M))
+        e_first = [ps.tile([P, BANK], F32, name="e0_%d" % i, tag="bank%d" % i) for i in range(3)]
+        e = {n: ps.tile([P, BANK], F32, name="e%d" % n, tag="bank%d" % (4 + n)) for n in range(1, 4)}
+        y = [tile([P, M], F32, "y%d" % n) for n in range(4)]
+        second_pass(e_first[0], 0, 0, 0, 256, True, False)
+        for n in range(1, 4):
             second_pass(e[n], n, 0, 0, 256, True, False)
-        second_pass(e_late, 0, 0, 256, M, True, False)
+        for i, (m0, m1) in enumerate(first_ranges):
+            if i > 0:
+                second_pass(e_first[i], 0, 0, m0, m1, True, False)
+        for i, (m0, m1) in enumerate(first_ranges):
+            second_pass(e_first[i], 0, 1, m0, m1, False, True)
+            nc.scalar.activation(y[0][:, m0:m1], e_first[i][:, m0:m1], SIGMOID)
         for n in range(1, 4):
+            second_pass(e[n], n, 1, 256, M, False, False)
             second_pass(e[n], n, 0, 256, M, False, False)
-        second_pass(e[0], 0, 1, 0, 256, False, True)
-        second_pass(e_late, 0, 1, 256, 384, False, False)
-        second_pass(e_late, 0, 1, 384, 512, False, True)
-        for n in range(1, 4):
-            second_pass(e[n], n, 1, 0, M, False, True)
+            second_pass(e[n], n, 1, 0, 256, False, True)
+            nc.scalar.activation(y[n][:], e[n][:], SIGMOID)
 
-        def pick_right(n):
-            y[n] = tile([P, M], F32, "y%d" % n)
-            if n == 0:
-                nc.scalar.activation(y[0][:, 0:256], e[0][:, 0:256], SIGMOID)
-                nc.scalar.activation(y[0][:, 256:M], e_late[:, 256:M], SIGMOID)
-            else:
-                nc.scalar.activation(y[n][:], e[n][:], SIGMOID)
+        halves = ((0, J // 2), (J // 2, J))
+        less = tile([P, J], F32, "less")
+        minus_res = tile([P, J], F32, "minus_res")
+        for j0, j1 in halves:
+            picked = y[0][:].indirect(pos4_t[:, j0 // 16 : j1 // 16])
+            nc.vector.tensor_tensor(less[:, j0:j1], picked, ones[:, j0:j1], SUBTRACT)
+        for j0, j1 in halves:
+            picked = y[0][:].indirect(pos3_t[:, j0 // 16 : j1 // 16])
+            nc.vector.tensor_tensor(minus_res[:, j0:j1], picked, less[:, j0:j1], MULT)
+        right, res = {}, {}
+        for n in range(1, 4):
             right[n] = tile([P, J], F32, "right%d" % n)
             nc.vector.tensor_copy(right[n][:], y[n][:].indirect(pos4_t[:]))
-
-        def finish(n):
+        for n in range(1, 4):
             not_right = tile([P, J], F32, "not_right%d" % n)
             nc.scalar.activation(not_right[:], right[n][:], COPY, bias=1.0, scale=-1.0)
-            res = tile([P, J], F32, "res%d" % n)
-            for j0, j1 in [(0, J)] if n < 3 else [(0, J // 2), (J // 2, J)]:
+            res[n] = tile([P, J], F32, "res%d" % n)
+            for j0, j1 in halves if n == 3 else ((0, J),):
                 picked = y[n][:].indirect(pos3_t[:, j0 // 16 : j1 // 16])
-                nc.vector.tensor_tensor(res[:, j0:j1], picked, not_right[:, j0:j1], MULT)
-                nc.sync.dma_start(out[P * n : P * (n + 1), j0:j1], res[:, j0:j1])
-
-        for n in range(3):
-            pick_right(n)
-        finish(0)
-        pick_right(3)
-        for n in range(1, 4):
-            finish(n)
+                nc.vector.tensor_tensor(res[n][:, j0:j1], picked, not_right[:, j0:j1], MULT)
+                nc.sync.dma_start(out[P * n : P * (n + 1), j0:j1], res[n][:, j0:j1])
+            if n == 1:
+                res[0] = tile([P, J], F32, "res0")
+                nc.scalar.activation(res[0][:], minus_res[:], COPY, scale=-1.0)
+                nc.sync.dma_start(out[0:P, :], res[0][:])

@@ -19,7 +19,7 @@ P = 128
 HALF = 64
 K, T, S, H, M, N, J = 1024, 2048, 1024, 1024, 512, 512, 256
 BANK = 512
-PARTS = ((0, 192), (192, 320), (320, 448), (448, 512))
+PARTS = ((0, 256), (256, 384), (384, 512))
 FLOPS = 2 * K * H * S + 2 * H * N * M
 
 
@@ -130,7 +130,7 @@ def tile_list_boolean_tree_retrieval_kernel(
         def first_pass(u, a, start):
             for s in range(2):
                 if start:
-                    banks[u, s] = ps.tile([P, BANK], F32, name="d%d%d" % (u, s), tag="bank%d" % (2 * (u if u < 4 else u % 2) + s))
+                    banks[u, s] = ps.tile([P, BANK], F32, name="d%d%d" % (u, s), tag="bank%d" % (2 * (u % 4) + s))
                 cols = slice(BANK * s, BANK * (s + 1))
                 nc.tensor.matmul_mx(
                     banks[u, s][:],
@@ -166,6 +166,17 @@ def tile_list_boolean_tree_retrieval_kernel(
         round_w1("q0", 0, None)
         quant_w1("q0", 0, None, 0)
         gather_words(1, 0, S)
+        unread_head = ps.tile([P, BANK], F32, name="unread_head", tag="bank7")
+        for i in range(2):
+            nc.tensor.matmul_mx(
+                unread_head[:, 0:512],
+                lhsT=w_code[0, 0].bitcast(FP8X4),
+                lhsT_scale=w_sc[0, 0],
+                rhs=v_w[0][:, 0:512].bitcast(FP8X4),
+                rhs_scale=picked_sc[:, 0:512],
+                start=True,
+                stop=True,
+            )
         first_pass(0, 0, True)
         for u in range(4, 8):
             spread_gain(u)
@@ -231,6 +242,8 @@ def tile_list_boolean_tree_retrieval_kernel(
         first_pass(5, 0, False)
         round_w1("hi", 0, 1, tag="w_code21")
         quant_w1("hi", 1, 1, 6)
+        for u in range(6, 8):
+            first_pass(u, 1, True)
         stage = tile([P, 2, M], F32, "stage", tag="rawhi1")
         for i in range(2):
             gather_right(2 + i, stage[:, i, :], 0, M)
@@ -239,8 +252,7 @@ def tile_list_boolean_tree_retrieval_kernel(
         sigmoid_h(4)
         sigmoid_h(5)
         for u in range(6, 8):
-            first_pass(u, 0, True)
-            first_pass(u, 1, False)
+            first_pass(u, 0, False)
             sigmoid_h(u)
         z_code = [tile([P, M], U32, "z_code%d" % a) for a in range(2)]
         z_sc = [tile([P, M], U8, "z_sc%d" % a) for a in range(2)]
@@ -250,10 +262,10 @@ def tile_list_boolean_tree_retrieval_kernel(
 
         gather_left(4)
         gather_left(5)
-        front = tile([P, 2, M], F32, "front", tag="w_sc61")
+        front = tile([P, 2, M], F32, "front", tag="w_sc60")
         for t in range(2):
             gather_right(4 + t, front[:, t, :], 0, M)
-        z_bf0 = tile([P, 4 * M], BF16, "z_bf0", tag="w_code61")
+        z_bf0 = tile([P, 4 * M], BF16, "z_bf0", tag="w_code60")
         nc.scalar.copy(
             z_bf0[:].rearrange("p (c i t) -> p c t i", i=4, t=4),
             z0[:].rearrange("p (t c i) -> p c t i", t=4, i=4),
@@ -276,7 +288,7 @@ def tile_list_boolean_tree_retrieval_kernel(
             weave_pair(1, part, m0, m1)
         quant_z(1, z_bf1, 0, 256)
         quant_z(0, z_bf0[:], 256, M)
-        for m0, m1 in ((256, 384), (384, 448), (448, 512)):
+        for m0, m1 in PARTS[1:]:
             quant_z(1, z_bf1, m0, m1)
 
         def second_pass(bank, n, a, m0, m1, start, stop):
@@ -297,6 +309,9 @@ def tile_list_boolean_tree_retrieval_kernel(
         second_pass(e_first[0], 0, 0, 0, 256, True, False)
         for n in range(1, 4):
             second_pass(e[n], n, 0, 0, 256, True, False)
+        unread = ps.tile([P, BANK], F32, name="unread", tag="bank4")
+        for i in range(4):
+            second_pass(unread, 0, 0, 0, 256, True, True)
         for i, (m0, m1) in enumerate(first_ranges):
             if i > 0:
                 second_pass(e_first[i], 0, 0, m0, m1, True, False)

@@ -19,6 +19,7 @@ P = 128
 HALF = 64
 K, T, S, H, M, N, J = 1024, 2048, 1024, 1024, 512, 512, 256
 BANK = 512
+EARLY = 768
 PARTS = ((0, 256), (256, 384), (384, 512))
 FLOPS = 2 * K * H * S + 2 * H * N * M
 
@@ -127,17 +128,22 @@ def tile_list_boolean_tree_retrieval_kernel(
 
         banks = {}
 
-        def first_pass(u, a, start):
-            for s in range(2):
+        def bank_ranges(u):
+            return ((0, 256), (256, EARLY), (EARLY, S)) if u == 0 else ((0, BANK), (BANK, S))
+
+        def first_pass(u, a, start, halves=None):
+            for s, (b0, b1) in enumerate(bank_ranges(u)):
+                if halves is not None and s not in halves:
+                    continue
                 if start:
-                    banks[u, s] = ps.tile([P, BANK], F32, name="d%d%d" % (u, s), tag="bank%d" % (2 * (u % 4) + s))
-                cols = slice(BANK * s, BANK * (s + 1))
+                    bank = 7 if s == 2 else 2 * (u % 4) + s
+                    banks[u, s] = ps.tile([P, BANK], F32, name="d%d%d" % (u, s), tag="bank%d" % bank)
                 nc.tensor.matmul_mx(
-                    banks[u, s][:],
+                    banks[u, s][:, 0 : b1 - b0],
                     lhsT=w_code[u, a].bitcast(FP8X4),
                     lhsT_scale=w_sc[u, a],
-                    rhs=v_w[a][:, cols].bitcast(FP8X4),
-                    rhs_scale=v_sc[4 * a : P, cols],
+                    rhs=v_w[a][:, b0:b1].bitcast(FP8X4),
+                    rhs_scale=v_sc[4 * a : P, b0:b1],
                     start=start,
                     stop=not start,
                 )
@@ -146,8 +152,8 @@ def tile_list_boolean_tree_retrieval_kernel(
 
         def sigmoid_h(u):
             h[u] = tile([P, S], F32, "h%d" % u)
-            for s in range(2):
-                nc.scalar.activation(h[u][:, BANK * s : BANK * (s + 1)], banks[u, s][:], SIGMOID)
+            for s, (b0, b1) in enumerate(bank_ranges(u)):
+                nc.scalar.activation(h[u][:, b0:b1], banks[u, s][:, 0 : b1 - b0], SIGMOID)
 
         z0 = tile([P, 4 * M], F32, "z0")
         spread = [tile([P, M], F32, "gain_row%d" % u)[:] for u in range(8)]
@@ -166,7 +172,7 @@ def tile_list_boolean_tree_retrieval_kernel(
         round_w1("q0", 0, None)
         quant_w1("q0", 0, None, 0)
         gather_words(1, 0, S)
-        unread_head = ps.tile([P, BANK], F32, name="unread_head", tag="bank7")
+        unread_head = ps.tile([P, BANK], F32, name="unread_head", tag="bank6")
         for i in range(2):
             nc.tensor.matmul_mx(
                 unread_head[:, 0:512],

from contextlib import ExitStack

import concourse.mybir as mybir

F32 = mybir.dt.float32
BF16 = mybir.dt.bfloat16
I32 = mybir.dt.int32
U32 = mybir.dt.uint32
U16 = mybir.dt.uint16
U8 = mybir.dt.uint8
FP8X4 = mybir.dt.float8_e4m3fn_x4
FP4X4 = mybir.dt.float4_e2m1fn_x4
MULT = mybir.AluOpType.mult
SUBTRACT = mybir.AluOpType.subtract
SIGMOID = mybir.ActivationFunctionType.Sigmoid
COPY = mybir.ActivationFunctionType.Copy

P = 128
HALF = 64
K, T, S, H, M, N, J = 1024, 2048, 1024, 1024, 512, 512, 256
BANK = 512
EARLY = 768
PARTS = ((0, 256), (256, 384), (384, 512))
FLOPS = 2 * K * H * S + 2 * H * N * M


def tile_list_boolean_tree_retrieval_kernel(
    tc, tab_words, tab_scales, w1, gain, w2_words, w2_scales, offs, pos1, pos2, pos3, pos4, out
):
    nc = tc.nc
    with ExitStack() as ctx:
        sb = ctx.enter_context(tc.tile_pool(name="sb", bufs=1))
        ps = ctx.enter_context(tc.psum_pool(name="ps", bufs=1))

        def tile(shape, dtype, name, tag=None):
            return sb.tile(shape, dtype, name=name, tag=tag or name, align_bytes=64)

        def load_list(src, name):
            t = sb.tile(list(src.shape), U16, name=name)
            nc.sync.dma_start(t[:], src)
            return t

        tab_sc = tile([P, T], U8, "tab_sc")
        nc.vector.memset(tab_sc[32:64, :].bitcast(I32), 0)
        nc.vector.memset(tab_sc[64:P, :].bitcast(I32), 0)
        v_sc = tile([P, S], U8, "v_sc")
        nc.vector.memset(v_sc[:].bitcast(I32), 0)
        w2_sc = tile([P, 2, N], U8, "w2_sc")
        nc.vector.memset(w2_sc[:].rearrange("p a n -> p (a n)").bitcast(I32), 0)

        ones = tile([P, J], F32, "ones")
        nc.vector.memset(ones[:], 1.0)

        tab_w = [tile([P, T], I32, "tab_w%d" % a) for a in range(2)]
        raw = {}

        def load_tab(a):
            nc.sync.dma_start(tab_w[a][:], tab_words[a].rearrange("p t i -> p (t i)").bitcast(I32))

        def load_w1(name, a, c0, c1):
            raw[name, a] = tile([P, 4, c1 - c0], F32, "raw%s%d" % (name, a))
            nc.sync.dma_start(raw[name, a][:], w1[512 * a : 512 * a + 512, c0:c1].rearrange("(p j) c -> p j c", j=4))

        gain_lo = tile([P, 2, 4], F32, "gain_lo")
        for half in range(2):
            shifted = gain[half : 512 + half].rearrange("(q p t) -> p q t", q=2, t=4)
            nc.scalar.dma_start(gain_lo[HALF * half : HALF * (half + 1), :, :], shifted)
        scale_rows = tab_scales.rearrange("a (q r) t -> r q a t", r=4)
        for r in range(4):
            nc.sync.dma_start(tab_sc[r:32:4, :].bitcast(I32), scale_rows[r].bitcast(I32))
        offs_t = load_list(offs, "offs_t")
        load_tab(0)
        load_w1("q0", 0, 0, 256)
        gain_hi = tile([P, 4], F32, "gain_hi")
        nc.sync.dma_start(gain_hi[:], gain[512:1024].rearrange("(p t) -> p t", t=4))
        pos1_t = load_list(pos1, "pos1_t")
        load_tab(1)
        load_w1("q0", 1, 0, 256)
        load_w1("q1", 0, 256, 512)
        load_w1("q1", 1, 256, 512)
        pos2_t = load_list(pos2, "pos2_t")
        load_w1("hi", 0, 512, 1024)
        load_w1("hi", 1, 512, 1024)
        w2_w = tile([P, 2, 2 * N], U8, "w2_w")
        nc.sync.dma_start(w2_w[:].bitcast(I32), w2_words.rearrange("a p c -> p a c").bitcast(I32))
        for q in range(4):
            nc.sync.dma_start(
                w2_sc[32 * q : 32 * q + 4, :, :].bitcast(I32),
                w2_scales[:, 4 * q : 4 * q + 4, :].rearrange("a r c -> r a c").bitcast(I32),
            )
        pos3_t = load_list(pos3, "pos3_t")
        pos4_t = load_list(pos4, "pos4_t")

        warm = tile([P, 2], F32, "warm")
        nc.gpsimd.memset(warm[:, 0:1], 0.0)
        nc.scalar.activation(warm[:, 1:2], warm[:, 0:1], SIGMOID)

        picked_sc = tile([P, S], U8, "picked_sc")
        v_w = [tile([P, S], U32, "v_w%d" % a) for a in range(2)]
        w_bf, w_code, w_sc = {}, {}, {}

        def gather_words(a, j0, j1):
            nc.vector.tensor_copy(v_w[a][:, j0:j1], tab_w[a][:].bitcast(U32).indirect(offs_t[:, j0 // 16 : j1 // 16]))

        def round_w1(name, a, u, on_vector=False, tag=None):
            width = raw[name, a].shape[2]
            src = raw[name, a][:].rearrange("p j (m u t) -> p u m j t", u=2, t=2)
            if u is None:
                w_bf[name, a, u] = tile([P, 4 * width], BF16, "w_bf%s%d" % (name, a), tag=tag)
                dst = w_bf[name, a, u][:].rearrange("p (u t m j) -> p u m j t", u=2, t=2, j=4)
            else:
                w_bf[name, a, u] = tile([P, 2 * width], BF16, "w_bf%s%d%d" % (name, a, u), tag=tag)
                dst = w_bf[name, a, u][:].rearrange("p (t m j) -> p m j t", t=2, j=4)
                src = src[:, u]
            if on_vector:
                nc.vector.tensor_copy(dst, src)
            else:
                nc.scalar.copy(dst, src)

        def quant_w1(name, a, u, first_tile):
            words = w_bf[name, a, u].shape[1] // 4
            code = tile([P, words], U32, "w_code%d%d" % (first_tile, a))
            scale = tile([P, words], U8, "w_sc%d%d" % (first_tile, a))
            nc.vector.quantize_mx(code[:].bitcast(FP8X4), scale[:], w_bf[name, a, u][:])
            for i in range(words // P):
                w_code[first_tile + i, a] = code[:, P * i : P * (i + 1)]
                w_sc[first_tile + i, a] = scale[:, P * i : P * (i + 1)]

        banks = {}

        def bank_ranges(u):
            return ((0, 256), (256, EARLY), (EARLY, S)) if u == 0 else ((0, BANK), (BANK, S))

        def first_pass(u, a, start, halves=None):
            for s, (b0, b1) in enumerate(bank_ranges(u)):
                if halves is not None and s not in halves:
                    continue
                if start:
                    bank = 7 if s == 2 else 2 * (u % 4) + s
                    banks[u, s] = ps.tile([P, BANK], F32, name="d%d%d" % (u, s), tag="bank%d" % bank)
                nc.tensor.matmul_mx(
                    banks[u, s][:, 0 : b1 - b0],
                    lhsT=w_code[u, a].bitcast(FP8X4),
                    lhsT_scale=w_sc[u, a],
                    rhs=v_w[a][:, b0:b1].bitcast(FP8X4),
                    rhs_scale=v_sc[4 * a : P, b0:b1],
                    start=start,
                    stop=not start,
                )

        h = {}

        def sigmoid_h(u):
            h[u] = tile([P, S], F32, "h%d" % u)
            for s, (b0, b1) in enumerate(bank_ranges(u)):
                nc.scalar.activation(h[u][:, b0:b1], banks[u, s][:, 0 : b1 - b0], SIGMOID)

        z0 = tile([P, 4 * M], F32, "z0")
        spread = [tile([P, M], F32, "gain_row%d" % u)[:] for u in range(8)]

        def spread_gain(u):
            col = gain_lo[:, u // 2, 2 * (u % 2) : 2 * (u % 2) + 1] if u < 4 else gain_hi[:, u - 4 : u - 3]
            nc.scalar.copy(spread[u], col.to_broadcast([P, M]))

        nc.vector.tensor_copy(picked_sc[:], tab_sc[:].indirect(offs_t[:]))
        for q in range(1, 4):
            nc.scalar.dma_start(v_sc[32 * q : 32 * q + 8, :].bitcast(I32), picked_sc[8 * q : 8 * q + 8, :].bitcast(I32))
        nc.vector.tensor_copy(v_sc[0:8, :].bitcast(I32), picked_sc[0:8, :].bitcast(I32))
        gather_words(0, 0, S)
        for u in range(4):
            spread_gain(u)
        round_w1("q0", 0, None)
        quant_w1("q0", 0, None, 0)
        gather_words(1, 0, S)
        unread_head = ps.tile([P, BANK], F32, name="unread_head", tag="bank6")
        for i in range(2):
            nc.tensor.matmul_mx(
                unread_head[:, 0:512],
                lhsT=w_code[0, 0].bitcast(FP8X4),
                lhsT_scale=w_sc[0, 0],
                rhs=v_w[0][:, 0:512].bitcast(FP8X4),
                rhs_scale=picked_sc[:, 0:512],
                start=True,
                stop=True,
            )
        first_pass(0, 0, True)
        for u in range(4, 8):
            spread_gain(u)
        for u in range(2):
            round_w1("q0", 1, u)
        quant_w1("q0", 1, 0, 0)
        first_pass(0, 1, False)
        round_w1("q1", 0, None, True)
        quant_w1("q0", 1, 1, 1)
        first_pass(1, 1, True)
        first_pass(1, 0, False)
        round_w1("q1", 1, 0, True)
        quant_w1("q1", 0, None, 2)
        for u in range(2, 4):
            first_pass(u, 0, True)

        left = {}

        def gather_left(u, m0=0, m1=M):
            if u not in left:
                left[u] = tile([P, M], F32, "left%d" % u)
            picked = h[u][:].indirect(pos1_t[:, m0 // 16 : m1 // 16])
            nc.vector.tensor_tensor(left[u][:, m0:m1], picked, spread[u][:, m0:m1], MULT)

        def gather_right(u, dst, m0, m1):
            nc.vector.tensor_tensor(dst, h[u][:].indirect(pos2_t[:, m0 // 16 : m1 // 16]), left[u][:, m0:m1], MULT)

        def plane(t):
            return z0[:, M * t : M * (t + 1)]

        def move_first(t):
            nc.sync.dma_start(plane(t + 1)[0:HALF, :], plane(t)[HALF:P, :])

        def move_second(t, src):
            nc.sync.dma_start(plane(t)[HALF:P, :], src[0:HALF, :])
            nc.sync.dma_start(plane(t + 1)[HALF:P, :], src[HALF:P, :])

        sigmoid_h(0)
        round_w1("q1", 1, 1)
        sigmoid_h(1)
        gather_left(0)
        quant_w1("q1", 1, 0, 2)
        first_pass(2, 1, False)
        gather_right(0, plane(0), 0, M)
        move_first(0)
        quant_w1("q1", 1, 1, 3)
        first_pass(3, 1, False)
        gather_left(1)
        gather_right(1, plane(2), 0, M)
        move_first(2)
        round_w1("hi", 0, 0)
        quant_w1("hi", 0, 0, 4)
        first_pass(4, 0, True)
        sigmoid_h(2)
        round_w1("hi", 1, 0, tag="w_code21")
        sigmoid_h(3)
        round_w1("hi", 1, 1)
        gather_left(2)
        gather_left(3)
        quant_w1("hi", 1, 0, 4)
        first_pass(4, 1, False)
        first_pass(5, 1, True)
        first_pass(5, 0, False)
        round_w1("hi", 0, 1, tag="w_code21")
        quant_w1("hi", 1, 1, 6)
        for u in range(6, 8):
            first_pass(u, 1, True)
        stage = tile([P, 2, M], F32, "stage", tag="rawhi1")
        for i in range(2):
            gather_right(2 + i, stage[:, i, :], 0, M)
            move_second(2 * i, stage[:, i, :])
        quant_w1("hi", 0, 1, 6)
        sigmoid_h(4)
        sigmoid_h(5)
        for u in range(6, 8):
            first_pass(u, 0, False)
            sigmoid_h(u)
        z_code = [tile([P, M], U32, "z_code%d" % a) for a in range(2)]
        z_sc = [tile([P, M], U8, "z_sc%d" % a) for a in range(2)]

        def quant_z(a, src, m0, m1):
            nc.vector.quantize_mx(z_code[a][:, m0:m1].bitcast(FP8X4), z_sc[a][:, m0:m1], src[:, 4 * m0 : 4 * m1])

        gather_left(4)
        gather_left(5)
        front = tile([P, 2, M], F32, "front", tag="w_sc60")
        for t in range(2):
            gather_right(4 + t, front[:, t, :], 0, M)
        z_bf0 = tile([P, 4 * M], BF16, "z_bf0", tag="w_code60")
        nc.scalar.copy(
            z_bf0[:].rearrange("p (c i t) -> p c t i", i=4, t=4),
            z0[:].rearrange("p (t c i) -> p c t i", t=4, i=4),
        )
        gather_left(6)
        gather_left(7)
        late = tile([P, 4 * M], F32, "late", tag="z0")
        z_bf1 = late[:, 0 : 2 * M].bitcast(BF16)

        def weave_pair(u, planes, m0, m1):
            dst = z_bf1[:, 4 * m0 : 4 * m1].rearrange("p (m u t) -> p u m t", u=2, t=2)
            nc.scalar.copy(dst[:, u], planes.rearrange("p t m -> p m t"))

        weave_pair(0, front[:], 0, M)
        quant_z(0, z_bf0[:], 0, 256)
        for m0, m1 in PARTS:
            part = late[:, 2 * (M + m0) : 2 * (M + m1)].rearrange("p (t m) -> p t m", t=2)
            for t in range(2):
                gather_right(6 + t, part[:, t, :], m0, m1)
            weave_pair(1, part, m0, m1)
        quant_z(1, z_bf1, 0, 256)
        quant_z(0, z_bf0[:], 256, M)
        for m0, m1 in PARTS[1:]:
            quant_z(1, z_bf1, m0, m1)

        def second_pass(bank, n, a, m0, m1, start, stop):
            nc.tensor.matmul_mx(
                bank[:, m0:m1],
                lhsT=w2_w[:, a, 256 * n : 256 * (n + 1)].bitcast(FP4X4),
                lhsT_scale=w2_sc[:, a, 128 * n : 128 * (n + 1)],
                rhs=z_code[a][:, m0:m1].bitcast(FP8X4),
                rhs_scale=z_sc[a][:, m0:m1],
                start=start,
                stop=stop,
            )

        first_ranges = ((0, 256), (256, 384), (384, M))
        e_first = [ps.tile([P, BANK], F32, name="e0_%d" % i, tag="bank%d" % i) for i in range(3)]
        e = {n: ps.tile([P, BANK], F32, name="e%d" % n, tag="bank%d" % (4 + n)) for n in range(1, 4)}
        y = [tile([P, M], F32, "y%d" % n) for n in range(4)]
        second_pass(e_first[0], 0, 0, 0, 256, True, False)
        for n in range(1, 4):
            second_pass(e[n], n, 0, 0, 256, True, False)
        unread = ps.tile([P, BANK], F32, name="unread", tag="bank4")
        for i in range(4):
            second_pass(unread, 0, 0, 0, 256, True, True)
        for i, (m0, m1) in enumerate(first_ranges):
            if i > 0:
                second_pass(e_first[i], 0, 0, m0, m1, True, False)
        for i, (m0, m1) in enumerate(first_ranges):
            second_pass(e_first[i], 0, 1, m0, m1, False, True)
            nc.scalar.activation(y[0][:, m0:m1], e_first[i][:, m0:m1], SIGMOID)
        for n in range(1, 4):
            second_pass(e[n], n, 1, 256, M, False, False)
            second_pass(e[n], n, 0, 256, M, False, False)
            second_pass(e[n], n, 1, 0, 256, False, True)
            nc.scalar.activation(y[n][:], e[n][:], SIGMOID)

        halves = ((0, J // 2), (J // 2, J))
        less = tile([P, J], F32, "less")
        minus_res = tile([P, J], F32, "minus_res")
        for j0, j1 in halves:
            picked = y[0][:].indirect(pos4_t[:, j0 // 16 : j1 // 16])
            nc.vector.tensor_tensor(less[:, j0:j1], picked, ones[:, j0:j1], SUBTRACT)
        for j0, j1 in halves:
            picked = y[0][:].indirect(pos3_t[:, j0 // 16 : j1 // 16])
            nc.vector.tensor_tensor(minus_res[:, j0:j1], picked, less[:, j0:j1], MULT)
        right, res = {}, {}
        for n in range(1, 4):
            right[n] = tile([P, J], F32, "right%d" % n)
            nc.vector.tensor_copy(right[n][:], y[n][:].indirect(pos4_t[:]))
        for n in range(1, 4):
            not_right = tile([P, J], F32, "not_right%d" % n)
            nc.scalar.activation(not_right[:], right[n][:], COPY, bias=1.0, scale=-1.0)
            res[n] = tile([P, J], F32, "res%d" % n)
            for j0, j1 in halves if n == 3 else ((0, J),):
                picked = y[n][:].indirect(pos3_t[:, j0 // 16 : j1 // 16])
                nc.vector.tensor_tensor(res[n][:, j0:j1], picked, not_right[:, j0:j1], MULT)
                nc.sync.dma_start(out[P * n : P * (n + 1), j0:j1], res[n][:, j0:j1])
            if n == 1:
                res[0] = tile([P, J], F32, "res0")
                nc.scalar.activation(res[0][:], minus_res[:], COPY, scale=-1.0)
                nc.sync.dma_start(out[0:P, :], res[0][:])
